import numpy as np
import ml_dtypes


def mxq(x, axis, fmt="e4m3"):
    dtype, down = {"e4m3": (ml_dtypes.float8_e4m3fn, 7), "e5m2": (ml_dtypes.float8_e5m2, 14)}[fmt]
    v = np.moveaxis(np.asarray(x, np.float32).astype(ml_dtypes.bfloat16).astype(np.float64), axis, -1)
    blocks = v.reshape(v.shape[:-1] + (-1, 32))
    amax = np.abs(blocks).max(-1, keepdims=True)
    byte = np.maximum(np.where(amax > 0, np.frexp(amax)[1] - 1 + 127, 0) - down, 1)
    scale = np.exp2(byte - 127.0)
    codes = (blocks / scale).astype(np.float32).astype(dtype).astype(np.float64)
    return np.moveaxis((codes * scale).reshape(v.shape), -1, axis)


WIDE = False


def mx_kscale(k):
    if not WIDE:
        return np.ones(k)
    levels = np.array([10, -10, 5, -5, 0])
    if k % 512:
        return np.exp2(np.random.permutation(np.resize(levels, k // 32))).repeat(32)
    a = np.empty((k // 512, 16))
    for p in range(k // 512):
        a[p, :8] = np.random.permutation(np.resize(levels, 8))
        for g in range(8):
            far = levels[np.abs(levels - a[p, g]) >= 10]
            a[p, g + 8] = far[np.random.randint(len(far))]
    return np.exp2(a.ravel()).repeat(32)


def f64(x):
    return np.asarray(x).astype(np.float64)


def striped(idx):
    return np.tile(idx.reshape(-1, 16).T, (8, 1)).astype(np.uint16)


def unstriped(offs):
    return offs[:16].T.reshape(-1).astype(np.int64)


def pack_weight(w):
    k, n = w.shape
    w = f64(np.asarray(w, np.float32).astype(ml_dtypes.bfloat16)).reshape(k // 32, 32, n)
    amax = np.abs(w).max(1)
    byte = np.clip(np.where(amax > 0, np.frexp(amax)[1] - 1 + 127 - 7, 1), 1, 254)
    scaled = (w * np.exp2(127.0 - byte)[:, None, :]).reshape(k, n).astype(np.float32)
    words = np.ascontiguousarray(scaled.reshape(k // 512, 128, 4, n).transpose(0, 1, 3, 2)).astype(ml_dtypes.float8_e4m3fn).view(np.uint8)
    return words, np.ascontiguousarray(byte.astype(np.uint8).reshape(k // 512, 16, n))


def unpack_weight(words, scales):
    g, p, n, _ = words.shape
    vals = np.ascontiguousarray(words).view(ml_dtypes.float8_e4m3fn).astype(np.float64) * np.repeat(np.exp2(scales.astype(np.float64) - 127.0), 8, axis=1)[..., None]
    return vals.transpose(0, 1, 3, 2).reshape(g * 512, n)


def planes(y):
    n, m = y.shape
    v = y.astype(np.float32).astype(ml_dtypes.bfloat16).astype(np.float64).reshape(n // 32, 32, m)
    top = np.abs(v).max(1)
    byte = np.clip(np.where(top > 0, np.frexp(top)[1] - 1 + 127 - 7, 1), 1, 254)
    codes = (v * np.exp2(127.0 - byte)[:, None, :]).reshape(n, m).astype(np.float32).astype(ml_dtypes.float8_e4m3fn).view(np.uint8)
    words = codes.reshape(n // 512, 128, 4, m).transpose(0, 1, 3, 2)
    return np.ascontiguousarray(words), np.ascontiguousarray(byte.astype(np.uint8).reshape(n // 512, 16, m))


def relu(v):
    return np.maximum(v, 0.0)


def sigmoid(v):
    return 1.0 / (1.0 + np.exp(-np.maximum(v, -700.0)))


K, T, S, H = 512, 1024, 512, 512


def setup_inputs():
    n = np.random.standard_normal
    s = mx_kscale(K)[:, None]
    u = mx_kscale(H)
    packed_xT = pack_weight(n((K, T)) * s)
    return {
        "x_words": packed_xT[0],
        "x_scales": packed_xT[1],
        "w1": (n((K, H)) / np.sqrt(K) / s * u).astype(np.float32),
        "w2": (n((H, H)) / np.sqrt(H) / u[:, None]).astype(np.float32),
        "offs": striped(np.random.permutation(T)[:S]),
    }


def reference(x_words, x_scales, w1, w2, offs):
    xq = unpack_weight(x_words, x_scales)[:, unstriped(offs)]
    h = relu(mxq(f64(w1), 0, "e4m3").T @ xq)
    g = sigmoid(mxq(f64(w2), 0, "e4m3").T @ mxq(h, 0, "e4m3"))
    out_0 = h * g
    return (out_0,) + planes(out_0)

@@ -1,0 +1,173 @@
+from contextlib import ExitStack
+
+import concourse.mybir as mybir
+
+K, T, S, H = 512, 1024, 512, 512
+FLOPS = 2 * 2 * K * H * S
+
+F32 = mybir.dt.float32
+BF16 = mybir.dt.bfloat16
+I32 = mybir.dt.int32
+U32 = mybir.dt.uint32
+U16 = mybir.dt.uint16
+U8 = mybir.dt.uint8
+FP8X4 = mybir.dt.float8_e4m3fn_x4
+ACT = mybir.ActivationFunctionType
+ALU = mybir.AluOpType
+
+P = 128
+PACK = 4
+HALF = 64
+CHUNK = 128
+CHUNKS = S // CHUNK
+
+
+def tile_picked_zgrn_relu_po_kernel(tc, x_words, x_scales, w1, w2, offs, out_0, out_1, out_2):
+    nc = tc.nc
+    with ExitStack() as ctx:
+        keep = ctx.enter_context(tc.tile_pool(name="keep", bufs=1))
+        psum = ctx.enter_context(tc.psum_pool(name="psum", bufs=1))
+
+        def sbuf(name, shape, dtype):
+            return keep.tile(shape, dtype, name=name, align_bytes=64)
+
+        offsets = keep.tile([P, S // 16], U16, name="offsets")
+        word_table = sbuf("word_table", [P, T], U32)
+        scale_table = sbuf("scale_table", [P, T], U8)
+        nc.sync.dma_start(offsets[:], offs)
+        nc.vector.memset(scale_table[:].bitcast(I32), 0)
+        nc.sync.dma_start(out=word_table[:].bitcast(I32), in_=x_words[0].rearrange("p n t -> p (n t)").bitcast(I32))
+        for q in range(4):
+            nc.sync.dma_start(out=scale_table[32 * q : 32 * q + 4, :].bitcast(I32), in_=x_scales[0, 4 * q : 4 * q + 4, :].bitcast(I32))
+
+        raw = {}
+        for name, w in (("w1", w1), ("w2", w2)):
+            rows = w.rearrange("(p j) c -> p j c", j=PACK)
+            for half in range(2):
+                raw[name, half] = sbuf(f"{name}_raw{half}", [P, PACK, H // 2], F32)
+                nc.sync.dma_start(out=raw[name, half][:], in_=rows[:, :, half * (H // 2) : (half + 1) * (H // 2)])
+
+        warm_in = sbuf("warm_in", [P, 1], F32)
+        warm_out = sbuf("warm_out", [P, 1], F32)
+        nc.vector.memset(warm_in[:], 0.0)
+        nc.scalar.activation(warm_out[:], warm_in[:], ACT.Sigmoid)
+
+        x_codes = sbuf("x_codes", [P, S], U32)
+        x_bytes = sbuf("x_bytes", [P, S], U8)
+        nc.vector.tensor_copy(x_bytes[:], scale_table[:].indirect(offsets[:]))
+        nc.vector.tensor_copy(x_codes[:], word_table[:].indirect(offsets[:]))
+
+        codes = {(n, t): sbuf(f"{n}_codes{t}", [P, P], U32) for n in ("w1", "w2") for t in range(PACK)}
+        scales = {(n, t): sbuf(f"{n}_scales{t}", [P, P], U8) for n in ("w1", "w2") for t in range(PACK)}
+        grouped = {}
+
+        def round_weights(name, half, pair, on_scalar):
+            dealt = sbuf(f"{name}_dealt{half}{pair}", [P, 2, HALF, PACK], BF16)
+            grouped[name, half, pair] = dealt
+            src = raw[name, half][:].rearrange("p j (m t) -> p m j t", t=PACK)[:, :, :, 2 * pair : 2 * pair + 2]
+            dst = dealt[:].rearrange("p t m j -> p m j t")
+            if on_scalar:
+                nc.scalar.copy(dst, src)
+            else:
+                nc.vector.tensor_copy(dst, src)
+
+        def quantize_weights(name, half, t):
+            cols = slice(half * HALF, (half + 1) * HALF)
+            nc.vector.quantize_mx(
+                out=codes[name, t][:, cols].bitcast(FP8X4),
+                scales=scales[name, t][:, cols],
+                in_=grouped[name, half, t // 2][:, t % 2].rearrange("p m j -> p (m j)"),
+            )
+
+        def product(name, bank, rhs_codes, rhs_scales):
+            for t in range(PACK):
+                nc.tensor.matmul_mx(
+                    out=bank[:, t, :],
+                    lhsT=codes[name, t][:].bitcast(FP8X4),
+                    lhsT_scale=scales[name, t][:],
+                    rhs=rhs_codes.bitcast(FP8X4),
+                    rhs_scale=rhs_scales,
+                    start=True,
+                    stop=True,
+                )
+
+        round_weights("w1", 0, 0, True)
+        round_weights("w1", 0, 1, True)
+        round_weights("w1", 1, 0, False)
+        round_weights("w1", 1, 1, True)
+        for half in range(2):
+            for t in range(PACK):
+                quantize_weights("w1", half, t)
+
+        pre = [psum.tile([P, PACK, CHUNK], F32, name=f"pre{c}") for c in range(CHUNKS)]
+        logits = [psum.tile([P, PACK, CHUNK], F32, name=f"logits{c}") for c in range(CHUNKS)]
+        h_bf = [sbuf(f"h_bf{c}", [P, CHUNK, PACK], BF16) for c in range(CHUNKS)]
+        h_codes = [sbuf(f"h_codes{c}", [P, CHUNK], U32) for c in range(CHUNKS)]
+        h_scales = [sbuf(f"h_scales{c}", [P, CHUNK], U8) for c in range(CHUNKS)]
+        gate = [sbuf(f"gate{c}", [P, PACK, CHUNK], F32) for c in range(CHUNKS)]
+        y = [sbuf(f"y{c}", [P, PACK, CHUNK], F32) for c in range(CHUNKS)]
+        y_bf = [sbuf(f"y_bf{c}", [P, CHUNK, PACK], BF16) for c in range(CHUNKS)]
+        y_codes = sbuf("y_codes", [P, S], U32)
+        y_scales = sbuf("y_scales", [P, S], U8)
+
+        for c in range(CHUNKS):
+            cols = slice(c * CHUNK, (c + 1) * CHUNK)
+            product("w1", pre[c], x_codes[:, cols], x_bytes[:, cols])
+
+        def round_hidden(c):
+            nc.scalar.activation(h_bf[c][:], pre[c][:].rearrange("p t n -> p n t"), ACT.Relu)
+
+        def quantize_hidden(c):
+            nc.vector.quantize_mx(out=h_codes[c][:].bitcast(FP8X4), scales=h_scales[c][:], in_=h_bf[c][:].rearrange("p n t -> p (n t)"))
+
+        round_weights("w2", 0, 0, False)
+        round_weights("w2", 0, 1, False)
+        round_hidden(0)
+        round_hidden(1)
+        for t in range(PACK):
+            quantize_weights("w2", 0, t)
+        quantize_hidden(0)
+        round_weights("w2", 1, 0, False)
+        round_weights("w2", 1, 1, True)
+        quantize_hidden(1)
+        for t in range(PACK):
+            quantize_weights("w2", 1, t)
+        round_hidden(2)
+        round_hidden(3)
+        quantize_hidden(2)
+        quantize_hidden(3)
+
+        y_rows = out_0.rearrange("(p t) n -> p t n", t=PACK)
+        word_rows = out_1[0].rearrange("p n t -> p (n t)").bitcast(I32)
+
+        def round_result(c, on_scalar):
+            dst = y_bf[c][:].rearrange("p (g i) t -> p g t i", i=4)
+            src = y[c][:].rearrange("p t (g i) -> p g t i", i=4)
+            if on_scalar:
+                nc.scalar.copy(dst, src)
+            else:
+                nc.vector.tensor_copy(dst, src)
+
+        def quantize_result(c):
+            cols = slice(c * CHUNK, (c + 1) * CHUNK)
+            nc.vector.quantize_mx(out=y_codes[:, cols].bitcast(FP8X4), scales=y_scales[:, cols], in_=y_bf[c][:].rearrange("p n t -> p (n t)"))
+
+        for c in range(CHUNKS):
+            product("w2", logits[c], h_codes[c][:], h_scales[c][:])
+        for c in range(CHUNKS):
+            nc.scalar.activation(gate[c][:], logits[c][:], ACT.Sigmoid)
+        for c in range(CHUNKS):
+            cols = slice(c * CHUNK, (c + 1) * CHUNK)
+            nc.vector.scalar_tensor_tensor(y[c][:], pre[c][:], 0.0, gate[c][:], ALU.max, ALU.mult)
+            nc.sync.dma_start(out=y_rows[:, :, cols], in_=y[c][:])
+            if c >= 1:
+                round_result(c - 1, c - 1 == 2)
+            if c >= 2:
+                quantize_result(c - 2)
+        round_result(CHUNKS - 1, False)
+        quantize_result(CHUNKS - 2)
+        quantize_result(CHUNKS - 1)
+        nc.sync.dma_start(out=word_rows, in_=y_codes[:].bitcast(I32))
+        for q in range(4):
+            queue = nc.scalar if q % 2 == 0 else nc.sync
+            queue.dma_start(out=out_2[0, 4 * q : 4 * q + 4, :].bitcast(I32), in_=y_scales[32 * q : 32 * q + 4, :].bitcast(I32))

@@ -28,8 +28,8 @@ def tile_picked_zgrn_relu_po_kernel(tc, x_words, x_scales, w1, w2, offs, out_0, 
         keep = ctx.enter_context(tc.tile_pool(name="keep", bufs=1))
         psum = ctx.enter_context(tc.psum_pool(name="psum", bufs=1))
 
-        def sbuf(name, shape, dtype):
-            return keep.tile(shape, dtype, name=name, align_bytes=64)
+        def sbuf(name, shape, dtype, tag=None):
+            return keep.tile(shape, dtype, name=name, tag=tag or name, align_bytes=64)
 
         offsets = keep.tile([P, S // 16], U16, name="offsets")
         word_table = sbuf("word_table", [P, T], U32)
@@ -53,23 +53,27 @@ def tile_picked_zgrn_relu_po_kernel(tc, x_words, x_scales, w1, w2, offs, out_0, 
         nc.scalar.activation(warm_out[:], warm_in[:], ACT.Sigmoid)
 
         x_codes = sbuf("x_codes", [P, S], U32)
-        x_bytes = sbuf("x_bytes", [P, S], U8)
-        nc.vector.tensor_copy(x_bytes[:], scale_table[:].indirect(offsets[:]))
         nc.vector.tensor_copy(x_codes[:], word_table[:].indirect(offsets[:]))
+        x_bytes = [sbuf("x_bytes0", [P, S // 2], U8)]
+        nc.vector.tensor_copy(x_bytes[0][:], scale_table[:].indirect(offsets[:, : S // 32]))
 
         codes = {(n, t): sbuf(f"{n}_codes{t}", [P, P], U32) for n in ("w1", "w2") for t in range(PACK)}
         scales = {(n, t): sbuf(f"{n}_scales{t}", [P, P], U8) for n in ("w1", "w2") for t in range(PACK)}
         grouped = {}
 
-        def round_weights(name, half, pair, on_scalar):
+        def round_copy(engine, dst, src):
+            if engine == "scalar":
+                nc.scalar.copy(dst, src)
+            elif engine == "vector":
+                nc.vector.tensor_copy(dst, src)
+            else:
+                nc.gpsimd.tensor_scalar(dst, src, 1.0, 0.0, ALU.mult, ALU.add)
+
+        def round_weights(name, half, pair, engine):
             dealt = sbuf(f"{name}_dealt{half}{pair}", [P, 2, HALF, PACK], BF16)
             grouped[name, half, pair] = dealt
             src = raw[name, half][:].rearrange("p j (m t) -> p m j t", t=PACK)[:, :, :, 2 * pair : 2 * pair + 2]
-            dst = dealt[:].rearrange("p t m j -> p m j t")
-            if on_scalar:
-                nc.scalar.copy(dst, src)
-            else:
-                nc.vector.tensor_copy(dst, src)
+            round_copy(engine, dealt[:].rearrange("p t m j -> p m j t"), src)
 
         def quantize_weights(name, half, t):
             cols = slice(half * HALF, (half + 1) * HALF)
@@ -91,17 +95,19 @@ def tile_picked_zgrn_relu_po_kernel(tc, x_words, x_scales, w1, w2, offs, out_0, 
                     stop=True,
                 )
 
-        round_weights("w1", 0, 0, True)
-        round_weights("w1", 0, 1, True)
-        round_weights("w1", 1, 0, False)
-        round_weights("w1", 1, 1, True)
+        round_weights("w1", 0, 0, "scalar")
+        round_weights("w1", 0, 1, "scalar")
+        round_weights("w1", 1, 0, "vector")
+        round_weights("w1", 1, 1, "scalar")
         for half in range(2):
             for t in range(PACK):
                 quantize_weights("w1", half, t)
+        x_bytes.append(sbuf("x_bytes1", [P, S // 2], U8, tag="w1_dealt11"))
+        nc.vector.tensor_copy(x_bytes[1][:], scale_table[:].indirect(offsets[:, S // 32 :]))
 
         pre = [psum.tile([P, PACK, CHUNK], F32, name=f"pre{c}") for c in range(CHUNKS)]
         logits = [psum.tile([P, PACK, CHUNK], F32, name=f"logits{c}") for c in range(CHUNKS)]
-        h_bf = [sbuf(f"h_bf{c}", [P, CHUNK, PACK], BF16) for c in range(CHUNKS)]
+        h_bf = {}
         h_codes = [sbuf(f"h_codes{c}", [P, CHUNK], U32) for c in range(CHUNKS)]
         h_scales = [sbuf(f"h_scales{c}", [P, CHUNK], U8) for c in range(CHUNKS)]
         gate = [sbuf(f"gate{c}", [P, PACK, CHUNK], F32) for c in range(CHUNKS)]
@@ -112,62 +118,72 @@ def tile_picked_zgrn_relu_po_kernel(tc, x_words, x_scales, w1, w2, offs, out_0, 
 
         for c in range(CHUNKS):
             cols = slice(c * CHUNK, (c + 1) * CHUNK)
-            product("w1", pre[c], x_codes[:, cols], x_bytes[:, cols])
+            product("w1", pre[c], x_codes[:, cols], x_bytes[c // 2][:, (c % 2) * CHUNK : (c % 2 + 1) * CHUNK])
 
-        def round_hidden(c):
-            nc.scalar.activation(h_bf[c][:], pre[c][:].rearrange("p t n -> p n t"), ACT.Relu)
+        def round_hidden(c, on_scalar):
+            h_bf[c] = sbuf(f"h_bf{c}", [P, CHUNK, PACK], BF16, tag=None if on_scalar else "w2_dealt10")
+            src = pre[c][:].rearrange("p t n -> p n t")
+            if on_scalar:
+                nc.scalar.activation(h_bf[c][:], src, ACT.Relu)
+            else:
+                nc.vector.tensor_scalar(h_bf[c][:], src, 0.0, None, ALU.max)
 
         def quantize_hidden(c):
             nc.vector.quantize_mx(out=h_codes[c][:].bitcast(FP8X4), scales=h_scales[c][:], in_=h_bf[c][:].rearrange("p n t -> p (n t)"))
 
-        round_weights("w2", 0, 0, False)
-        round_weights("w2", 0, 1, False)
-        round_hidden(0)
-        round_hidden(1)
-        for t in range(PACK):
-            quantize_weights("w2", 0, t)
-        quantize_hidden(0)
-        round_weights("w2", 1, 0, False)
-        round_weights("w2", 1, 1, True)
-        quantize_hidden(1)
-        for t in range(PACK):
-            quantize_weights("w2", 1, t)
-        round_hidden(2)
-        round_hidden(3)
-        quantize_hidden(2)
-        quantize_hidden(3)
-
         y_rows = out_0.rearrange("(p t) n -> p t n", t=PACK)
         word_rows = out_1[0].rearrange("p n t -> p (n t)").bitcast(I32)
 
-        def round_result(c, on_scalar):
+        def round_result(c, engine):
             dst = y_bf[c][:].rearrange("p (g i) t -> p g t i", i=4)
             src = y[c][:].rearrange("p t (g i) -> p g t i", i=4)
-            if on_scalar:
-                nc.scalar.copy(dst, src)
-            else:
-                nc.vector.tensor_copy(dst, src)
+            round_copy(engine, dst, src)
 
         def quantize_result(c):
             cols = slice(c * CHUNK, (c + 1) * CHUNK)
             nc.vector.quantize_mx(out=y_codes[:, cols].bitcast(FP8X4), scales=y_scales[:, cols], in_=y_bf[c][:].rearrange("p n t -> p (n t)"))
 
-        for c in range(CHUNKS):
+        def gate_chunk(c):
             product("w2", logits[c], h_codes[c][:], h_scales[c][:])
-        for c in range(CHUNKS):
             nc.scalar.activation(gate[c][:], logits[c][:], ACT.Sigmoid)
-        for c in range(CHUNKS):
-            cols = slice(c * CHUNK, (c + 1) * CHUNK)
+
+        def result_chunk(c):
             nc.vector.scalar_tensor_tensor(y[c][:], pre[c][:], 0.0, gate[c][:], ALU.max, ALU.mult)
-            nc.sync.dma_start(out=y_rows[:, :, cols], in_=y[c][:])
-            if c >= 1:
-                round_result(c - 1, c - 1 == 2)
-            if c >= 2:
-                quantize_result(c - 2)
-        round_result(CHUNKS - 1, False)
-        quantize_result(CHUNKS - 2)
-        quantize_result(CHUNKS - 1)
-        nc.sync.dma_start(out=word_rows, in_=y_codes[:].bitcast(I32))
+            nc.sync.dma_start(out=y_rows[:, :, c * CHUNK : (c + 1) * CHUNK], in_=y[c][:])
+
+        round_weights("w2", 0, 1, "scalar")
+        round_weights("w2", 0, 0, "vector")
+        round_hidden(0, True)
+        for t in range(PACK):
+            quantize_weights("w2", 0, t)
+        round_weights("w2", 1, 1, "scalar")
+        round_weights("w2", 1, 0, "vector")
+        quantize_hidden(0)
+        for t in range(PACK):
+            quantize_weights("w2", 1, t)
+        round_hidden(1, True)
+        round_hidden(2, False)
+        quantize_hidden(1)
+        quantize_hidden(2)
+        gate_chunk(0)
+        round_hidden(3, True)
+        result_chunk(0)
+        quantize_hidden(3)
+        gate_chunk(1)
+        result_chunk(1)
+        gate_chunk(2)
+        result_chunk(2)
+        gate_chunk(3)
+        result_chunk(3)
+        round_result(0, "vector")
+        round_result(1, "scalar")
+        round_result(2, "scalar")
+        round_result(3, "vector")
+        for c in range(CHUNKS):
+            quantize_result(c)
+            if c % 2 == 1:
+                cols = slice((c - 1) * CHUNK, (c + 1) * CHUNK)
+                nc.sync.dma_start(out=word_rows[:, cols], in_=y_codes[:, cols].bitcast(I32))
         for q in range(4):
             queue = nc.scalar if q % 2 == 0 else nc.sync
             queue.dma_start(out=out_2[0, 4 * q : 4 * q + 4, :].bitcast(I32), in_=y_scales[32 * q : 32 * q + 4, :].bitcast(I32))

@@ -20,6 +20,8 @@ PACK = 4
 HALF = 64
 CHUNK = 128
 CHUNKS = S // CHUNK
+PAIR = 2 * CHUNK
+W1_ON_SCALAR = 96
 
 
 def tile_picked_zgrn_relu_po_kernel(tc, x_words, x_scales, w1, w2, offs, out_0, out_1, out_2):
@@ -34,156 +36,197 @@ def tile_picked_zgrn_relu_po_kernel(tc, x_words, x_scales, w1, w2, offs, out_0, 
         offsets = keep.tile([P, S // 16], U16, name="offsets")
         word_table = sbuf("word_table", [P, T], U32)
         scale_table = sbuf("scale_table", [P, T], U8)
-        nc.sync.dma_start(offsets[:], offs)
+        w1_raw = sbuf("w1_raw", [P, PACK, H], F32)
+        w1_rows = w1.rearrange("(p j) c -> p j c", j=PACK)
+        w2_rows = w2.rearrange("(p j) c -> p j c", j=PACK)
         nc.vector.memset(scale_table[:].bitcast(I32), 0)
-        nc.sync.dma_start(out=word_table[:].bitcast(I32), in_=x_words[0].rearrange("p n t -> p (n t)").bitcast(I32))
+        nc.sync.dma_start(out=w1_raw[:, 0:2, :], in_=w1_rows[:, 0:2, :])
+        nc.sync.dma_start(offsets[:], offs)
         for q in range(4):
             nc.sync.dma_start(out=scale_table[32 * q : 32 * q + 4, :].bitcast(I32), in_=x_scales[0, 4 * q : 4 * q + 4, :].bitcast(I32))
-
-        raw = {}
-        for name, w in (("w1", w1), ("w2", w2)):
-            rows = w.rearrange("(p j) c -> p j c", j=PACK)
-            for half in range(2):
-                raw[name, half] = sbuf(f"{name}_raw{half}", [P, PACK, H // 2], F32)
-                nc.sync.dma_start(out=raw[name, half][:], in_=rows[:, :, half * (H // 2) : (half + 1) * (H // 2)])
+        nc.sync.dma_start(out=w1_raw[:, 2:4, :], in_=w1_rows[:, 2:4, :])
+        nc.sync.dma_start(out=word_table[:].bitcast(I32), in_=x_words[0].rearrange("p n t -> p (n t)").bitcast(I32))
+        w2_raw = []
+        for half in range(2):
+            w2_raw.append(sbuf(f"w2_raw{half}", [P, PACK, H // 2], F32))
+            nc.sync.dma_start(out=w2_raw[half][:], in_=w2_rows[:, :, half * (H // 2) : (half + 1) * (H // 2)])
 
         warm_in = sbuf("warm_in", [P, 1], F32)
         warm_out = sbuf("warm_out", [P, 1], F32)
         nc.vector.memset(warm_in[:], 0.0)
         nc.scalar.activation(warm_out[:], warm_in[:], ACT.Sigmoid)
 
-        x_codes = sbuf("x_codes", [P, S], U32)
-        nc.vector.tensor_copy(x_codes[:], word_table[:].indirect(offsets[:]))
-        x_bytes = [sbuf("x_bytes0", [P, S // 2], U8)]
-        nc.vector.tensor_copy(x_bytes[0][:], scale_table[:].indirect(offsets[:, : S // 32]))
-
-        codes = {(n, t): sbuf(f"{n}_codes{t}", [P, P], U32) for n in ("w1", "w2") for t in range(PACK)}
-        scales = {(n, t): sbuf(f"{n}_scales{t}", [P, P], U8) for n in ("w1", "w2") for t in range(PACK)}
-        grouped = {}
+        x_bytes = sbuf("x_bytes", [P, S], U8)
+        nc.vector.tensor_copy(x_bytes[:], scale_table[:].indirect(offsets[:]))
 
         def round_copy(engine, dst, src):
             if engine == "scalar":
                 nc.scalar.copy(dst, src)
-            elif engine == "vector":
-                nc.vector.tensor_copy(dst, src)
             else:
-                nc.gpsimd.tensor_scalar(dst, src, 1.0, 0.0, ALU.mult, ALU.add)
+                nc.vector.tensor_copy(dst, src)
 
-        def round_weights(name, half, pair, engine):
-            dealt = sbuf(f"{name}_dealt{half}{pair}", [P, 2, HALF, PACK], BF16)
-            grouped[name, half, pair] = dealt
-            src = raw[name, half][:].rearrange("p j (m t) -> p m j t", t=PACK)[:, :, :, 2 * pair : 2 * pair + 2]
-            round_copy(engine, dealt[:].rearrange("p t m j -> p m j t"), src)
+        def quantize(codes, scales, values):
+            nc.vector.quantize_mx(out=codes.bitcast(FP8X4), scales=scales, in_=values)
 
-        def quantize_weights(name, half, t):
-            cols = slice(half * HALF, (half + 1) * HALF)
-            nc.vector.quantize_mx(
-                out=codes[name, t][:, cols].bitcast(FP8X4),
-                scales=scales[name, t][:, cols],
-                in_=grouped[name, half, t // 2][:, t % 2].rearrange("p m j -> p (m j)"),
+        def product(out, w_codes, w_scales, a_codes, a_scales):
+            nc.tensor.matmul_mx(
+                out=out,
+                lhsT=w_codes.bitcast(FP8X4),
+                lhsT_scale=w_scales,
+                rhs=a_codes.bitcast(FP8X4),
+                rhs_scale=a_scales,
+                start=True,
+                stop=True,
             )
 
-        def product(name, bank, rhs_codes, rhs_scales):
-            for t in range(PACK):
-                nc.tensor.matmul_mx(
-                    out=bank[:, t, :],
-                    lhsT=codes[name, t][:].bitcast(FP8X4),
-                    lhsT_scale=scales[name, t][:],
-                    rhs=rhs_codes.bitcast(FP8X4),
-                    rhs_scale=rhs_scales,
-                    start=True,
-                    stop=True,
-                )
+        w1_dealt = [sbuf(f"w1_dealt{duo}", [P, 2, P, PACK], BF16) for duo in range(2)]
+        w1_codes = [sbuf(f"w1_codes{duo}", [P, 2, P], U32) for duo in range(2)]
+        w1_scales = [sbuf(f"w1_scales{duo}", [P, 2, P], U8) for duo in range(2)]
 
-        round_weights("w1", 0, 0, "scalar")
-        round_weights("w1", 0, 1, "scalar")
-        round_weights("w1", 1, 0, "vector")
-        round_weights("w1", 1, 1, "scalar")
-        for half in range(2):
-            for t in range(PACK):
-                quantize_weights("w1", half, t)
-        x_bytes.append(sbuf("x_bytes1", [P, S // 2], U8, tag="w1_dealt11"))
-        nc.vector.tensor_copy(x_bytes[1][:], scale_table[:].indirect(offsets[:, S // 32 :]))
+        def round_w1(duo, lo, hi, engine):
+            src = w1_raw[:].rearrange("p j (m t) -> p m j t", t=PACK)[:, lo:hi, :, 2 * duo : 2 * duo + 2]
+            round_copy(engine, w1_dealt[duo][:].rearrange("p t m j -> p m j t")[:, lo:hi], src)
+
+        def quantize_w1(duo):
+            quantize(
+                w1_codes[duo][:].rearrange("p t m -> p (t m)"),
+                w1_scales[duo][:].rearrange("p t m -> p (t m)"),
+                w1_dealt[duo][:].rearrange("p t m j -> p (t m j)"),
+            )
+
+        x_codes = sbuf("x_codes", [P, S], U32)
+
+        def gather_words(lo, hi):
+            nc.vector.tensor_copy(x_codes[:, lo:hi], word_table[:].indirect(offsets[:, lo // 16 : hi // 16]))
+
+        round_w1(0, 0, P, "vector")
+        round_w1(1, 0, W1_ON_SCALAR, "scalar")
+        round_w1(1, W1_ON_SCALAR, P, "vector")
+        quantize_w1(0)
+        gather_words(0, CHUNK)
+        quantize_w1(1)
+        gather_words(CHUNK, PAIR)
+        gather_words(PAIR, S)
 
         pre = [psum.tile([P, PACK, CHUNK], F32, name=f"pre{c}") for c in range(CHUNKS)]
-        logits = [psum.tile([P, PACK, CHUNK], F32, name=f"logits{c}") for c in range(CHUNKS)]
-        h_bf = {}
-        h_codes = [sbuf(f"h_codes{c}", [P, CHUNK], U32) for c in range(CHUNKS)]
-        h_scales = [sbuf(f"h_scales{c}", [P, CHUNK], U8) for c in range(CHUNKS)]
-        gate = [sbuf(f"gate{c}", [P, PACK, CHUNK], F32) for c in range(CHUNKS)]
-        y = [sbuf(f"y{c}", [P, PACK, CHUNK], F32) for c in range(CHUNKS)]
-        y_bf = [sbuf(f"y_bf{c}", [P, CHUNK, PACK], BF16) for c in range(CHUNKS)]
+        for c in range(CHUNKS):
+            cols = slice(c * CHUNK, (c + 1) * CHUNK)
+            for t in range(PACK):
+                product(pre[c][:, t, :], w1_codes[t // 2][:, t % 2, :], w1_scales[t // 2][:, t % 2, :], x_codes[:, cols], x_bytes[:, cols])
+
+        w2_codes = [sbuf(f"w2_codes{t}", [P, P], U32) for t in range(PACK)]
+        w2_scales = [sbuf(f"w2_scales{t}", [P, P], U8) for t in range(PACK)]
+        w2_dealt = {}
+
+        def round_w2(half, duo):
+            w2_dealt[half, duo] = sbuf(f"w2_dealt{half}{duo}", [P, 2, HALF, PACK], BF16)
+            src = w2_raw[half][:].rearrange("p j (m t) -> p m j t", t=PACK)[:, :, :, 2 * duo : 2 * duo + 2]
+            nc.vector.tensor_copy(w2_dealt[half, duo][:].rearrange("p t m j -> p m j t"), src)
+
+        def quantize_w2(half, t):
+            cols = slice(half * HALF, (half + 1) * HALF)
+            quantize(w2_codes[t][:, cols], w2_scales[t][:, cols], w2_dealt[half, t // 2][:, t % 2].rearrange("p m j -> p (m j)"))
+
+        h_bf = sbuf("h_bf", [P, S, PACK], BF16)
+        h_codes = {}
+        h_scales = {}
+        y = [sbuf(f"y{g}", [P, PACK, PAIR], F32) for g in range(2)]
+        y_bf = sbuf("y_bf", [P, S, PACK], BF16)
         y_codes = sbuf("y_codes", [P, S], U32)
         y_scales = sbuf("y_scales", [P, S], U8)
 
-        for c in range(CHUNKS):
-            cols = slice(c * CHUNK, (c + 1) * CHUNK)
-            product("w1", pre[c], x_codes[:, cols], x_bytes[c // 2][:, (c % 2) * CHUNK : (c % 2 + 1) * CHUNK])
+        def round_hidden(c):
+            nc.scalar.activation(h_bf[:, c * CHUNK : (c + 1) * CHUNK, :], pre[c][:].rearrange("p t n -> p n t"), ACT.Relu)
 
-        def round_hidden(c, on_scalar):
-            h_bf[c] = sbuf(f"h_bf{c}", [P, CHUNK, PACK], BF16, tag=None if on_scalar else "w2_dealt10")
-            src = pre[c][:].rearrange("p t n -> p n t")
-            if on_scalar:
-                nc.scalar.activation(h_bf[c][:], src, ACT.Relu)
-            else:
-                nc.vector.tensor_scalar(h_bf[c][:], src, 0.0, None, ALU.max)
-
-        def quantize_hidden(c):
-            nc.vector.quantize_mx(out=h_codes[c][:].bitcast(FP8X4), scales=h_scales[c][:], in_=h_bf[c][:].rearrange("p n t -> p (n t)"))
+        def quantize_hidden(first, count, slot):
+            codes = sbuf(f"h_codes{first}", [P, count * CHUNK], U32, tag=slot)
+            scales = sbuf(f"h_scales{first}", [P, count * CHUNK], U8)
+            quantize(codes[:], scales[:], h_bf[:, first * CHUNK : (first + count) * CHUNK, :].rearrange("p n t -> p (n t)"))
+            for n in range(1, count + 1):
+                for i in range(count - n + 1):
+                    h_codes[first + i, n] = codes[:, i * CHUNK : (i + n) * CHUNK]
+                    h_scales[first + i, n] = scales[:, i * CHUNK : (i + n) * CHUNK]
 
         y_rows = out_0.rearrange("(p t) n -> p t n", t=PACK)
         word_rows = out_1[0].rearrange("p n t -> p (n t)").bitcast(I32)
 
-        def round_result(c, engine):
-            dst = y_bf[c][:].rearrange("p (g i) t -> p g t i", i=4)
-            src = y[c][:].rearrange("p t (g i) -> p g t i", i=4)
+        def gate_and_result(duo, first, count, width, bank):
+            logits = psum.tile([P, 2, count * CHUNK], F32, name=f"logits{duo}{first}", tag=bank)
+            for lo in range(0, count, width):
+                for i in range(2):
+                    t = 2 * duo + i
+                    product(
+                        logits[:, i, lo * CHUNK : (lo + width) * CHUNK],
+                        w2_codes[t][:],
+                        w2_scales[t][:],
+                        h_codes[first + lo, width],
+                        h_scales[first + lo, width],
+                    )
+            gate = sbuf(f"gate{duo}{first}", [P, 2, count * CHUNK], F32)
+            nc.scalar.activation(gate[:], logits[:], ACT.Sigmoid)
+            ts = slice(2 * duo, 2 * duo + 2)
+            for i in range(count):
+                c = first + i
+                nc.vector.scalar_tensor_tensor(
+                    y[c // 2][:, ts, (c % 2) * CHUNK : (c % 2 + 1) * CHUNK],
+                    pre[c][:, ts, :],
+                    0.0,
+                    gate[:, :, i * CHUNK : (i + 1) * CHUNK],
+                    ALU.max,
+                    ALU.mult,
+                )
+
+        def store_result(duo, g):
+            ts = slice(2 * duo, 2 * duo + 2)
+            nc.sync.dma_start(out=y_rows[:, ts, g * PAIR : (g + 1) * PAIR], in_=y[g][:, ts, :])
+
+        def round_result(first, count, engine):
+            lo = (first % 2) * CHUNK
+            dst = y_bf[:, first * CHUNK : (first + count) * CHUNK, :].rearrange("p (g i) t -> p g t i", i=4)
+            src = y[first // 2][:, :, lo : lo + count * CHUNK].rearrange("p t (g i) -> p g t i", i=4)
             round_copy(engine, dst, src)
 
-        def quantize_result(c):
-            cols = slice(c * CHUNK, (c + 1) * CHUNK)
-            nc.vector.quantize_mx(out=y_codes[:, cols].bitcast(FP8X4), scales=y_scales[:, cols], in_=y_bf[c][:].rearrange("p n t -> p (n t)"))
+        def quantize_result(first, count):
+            cols = slice(first * CHUNK, (first + count) * CHUNK)
+            quantize(y_codes[:, cols], y_scales[:, cols], y_bf[:, cols, :].rearrange("p n t -> p (n t)"))
 
-        def gate_chunk(c):
-            product("w2", logits[c], h_codes[c][:], h_scales[c][:])
-            nc.scalar.activation(gate[c][:], logits[c][:], ACT.Sigmoid)
+        def store_codes(g):
+            cols = slice(g * PAIR, (g + 1) * PAIR)
+            nc.sync.dma_start(out=word_rows[:, cols], in_=y_codes[:, cols].bitcast(I32))
 
-        def result_chunk(c):
-            nc.vector.scalar_tensor_tensor(y[c][:], pre[c][:], 0.0, gate[c][:], ALU.max, ALU.mult)
-            nc.sync.dma_start(out=y_rows[:, :, c * CHUNK : (c + 1) * CHUNK], in_=y[c][:])
-
-        round_weights("w2", 0, 1, "scalar")
-        round_weights("w2", 0, 0, "vector")
-        round_hidden(0, True)
-        for t in range(PACK):
-            quantize_weights("w2", 0, t)
-        round_weights("w2", 1, 1, "scalar")
-        round_weights("w2", 1, 0, "vector")
-        quantize_hidden(0)
-        for t in range(PACK):
-            quantize_weights("w2", 1, t)
-        round_hidden(1, True)
-        round_hidden(2, False)
-        quantize_hidden(1)
-        quantize_hidden(2)
-        gate_chunk(0)
-        round_hidden(3, True)
-        result_chunk(0)
-        quantize_hidden(3)
-        gate_chunk(1)
-        result_chunk(1)
-        gate_chunk(2)
-        result_chunk(2)
-        gate_chunk(3)
-        result_chunk(3)
-        round_result(0, "vector")
-        round_result(1, "scalar")
-        round_result(2, "scalar")
-        round_result(3, "vector")
         for c in range(CHUNKS):
-            quantize_result(c)
-            if c % 2 == 1:
-                cols = slice((c - 1) * CHUNK, (c + 1) * CHUNK)
-                nc.sync.dma_start(out=word_rows[:, cols], in_=y_codes[:, cols].bitcast(I32))
+            round_hidden(c)
+        round_w2(0, 0)
+        round_w2(0, 1)
+        for t in range(PACK):
+            quantize_w2(0, t)
+        quantize_hidden(0, 1, "w2_raw0")
+        round_w2(1, 0)
+        round_w2(1, 1)
+        quantize_w2(1, 0)
+        quantize_w2(1, 1)
+        quantize_hidden(1, 1, "w2_raw1")
+        quantize_w2(1, 2)
+        quantize_w2(1, 3)
+        quantize_hidden(2, 2, "w2_dealt10")
+        gate_and_result(0, 0, 1, 1, "logits_a")
+        gate_and_result(0, 1, 1, 1, "logits_b")
+        store_result(0, 0)
+        gate_and_result(1, 0, 2, 1, "logits_c")
+        store_result(1, 0)
+        gate_and_result(0, 2, 2, 2, "logits_d")
+        store_result(0, 1)
+        gate_and_result(1, 2, 1, 1, "logits_a")
+        gate_and_result(1, 3, 1, 1, "logits_b")
+        store_result(1, 1)
+        round_result(0, 2, "scalar")
+        round_result(2, 1, "vector")
+        round_result(3, 1, "vector")
+        quantize_result(2, 1)
+        quantize_result(0, 2)
+        store_codes(0)
+        quantize_result(3, 1)
+        store_codes(1)
         for q in range(4):
             queue = nc.scalar if q % 2 == 0 else nc.sync
             queue.dma_start(out=out_2[0, 4 * q : 4 * q + 4, :].bitcast(I32), in_=y_scales[32 * q : 32 * q + 4, :].bitcast(I32))

@@ -182,9 +182,12 @@ def tile_picked_zgrn_relu_po_kernel(tc, x_words, x_scales, w1, w2, offs, out_0, 
 
         def round_result(first, count, engine):
             lo = (first % 2) * CHUNK
-            dst = y_bf[:, first * CHUNK : (first + count) * CHUNK, :].rearrange("p (g i) t -> p g t i", i=4)
-            src = y[first // 2][:, :, lo : lo + count * CHUNK].rearrange("p t (g i) -> p g t i", i=4)
-            round_copy(engine, dst, src)
+            dst = y_bf[:, first * CHUNK : (first + count) * CHUNK, :]
+            src = y[first // 2][:, :, lo : lo + count * CHUNK]
+            if engine == "gpsimd":
+                nc.gpsimd.tensor_scalar(dst, src.rearrange("p t n -> p n t"), 1.0, 0.0, ALU.mult, ALU.add)
+            else:
+                round_copy(engine, dst.rearrange("p (g i) t -> p g t i", i=4), src.rearrange("p t (g i) -> p g t i", i=4))
 
         def quantize_result(first, count):
             cols = slice(first * CHUNK, (first + count) * CHUNK)
@@ -219,13 +222,15 @@ def tile_picked_zgrn_relu_po_kernel(tc, x_words, x_scales, w1, w2, offs, out_0, 
         gate_and_result(1, 2, 1, 1, "logits_a")
         gate_and_result(1, 3, 1, 1, "logits_b")
         store_result(1, 1)
-        round_result(0, 2, "scalar")
-        round_result(2, 1, "vector")
+        round_result(0, 1, "gpsimd")
+        round_result(1, 1, "scalar")
+        round_result(2, 1, "scalar")
+        quantize_result(0, 1)
         round_result(3, 1, "vector")
-        quantize_result(2, 1)
-        quantize_result(0, 2)
+        quantize_result(1, 1)
         store_codes(0)
         quantize_result(3, 1)
+        quantize_result(2, 1)
         store_codes(1)
         for q in range(4):
             queue = nc.scalar if q % 2 == 0 else nc.sync

@@ -22,6 +22,7 @@ CHUNK = 128
 CHUNKS = S // CHUNK
 PAIR = 2 * CHUNK
 W1_ON_SCALAR = 96
+W2_EARLY = 80
 
 
 def tile_picked_zgrn_relu_po_kernel(tc, x_words, x_scales, w1, w2, offs, out_0, out_1, out_2):
@@ -47,9 +48,10 @@ def tile_picked_zgrn_relu_po_kernel(tc, x_words, x_scales, w1, w2, offs, out_0, 
         nc.sync.dma_start(out=w1_raw[:, 2:4, :], in_=w1_rows[:, 2:4, :])
         nc.sync.dma_start(out=word_table[:].bitcast(I32), in_=x_words[0].rearrange("p n t -> p (n t)").bitcast(I32))
         w2_raw = []
-        for half in range(2):
-            w2_raw.append(sbuf(f"w2_raw{half}", [P, PACK, H // 2], F32))
-            nc.sync.dma_start(out=w2_raw[half][:], in_=w2_rows[:, :, half * (H // 2) : (half + 1) * (H // 2)])
+        w2_parts = [(0, W2_EARLY), (W2_EARLY, P)]
+        for part, (lo, hi) in enumerate(w2_parts):
+            w2_raw.append(sbuf(f"w2_raw{part}", [P, PACK, (hi - lo) * PACK], F32))
+            nc.sync.dma_start(out=w2_raw[part][:], in_=w2_rows[:, :, lo * PACK : hi * PACK])
 
         warm_in = sbuf("warm_in", [P, 1], F32)
         warm_out = sbuf("warm_out", [P, 1], F32)
@@ -114,18 +116,21 @@ def tile_picked_zgrn_relu_po_kernel(tc, x_words, x_scales, w1, w2, offs, out_0, 
             for t in range(PACK):
                 product(pre[c][:, t, :], w1_codes[t // 2][:, t % 2, :], w1_scales[t // 2][:, t % 2, :], x_codes[:, cols], x_bytes[:, cols])
 
-        w2_codes = [sbuf(f"w2_codes{t}", [P, P], U32) for t in range(PACK)]
-        w2_scales = [sbuf(f"w2_scales{t}", [P, P], U8) for t in range(PACK)]
-        w2_dealt = {}
+        w2_dealt = [sbuf(f"w2_dealt{duo}", [P, 2, P, PACK], BF16) for duo in range(2)]
+        w2_codes = [sbuf(f"w2_codes{duo}", [P, 2, P], U32) for duo in range(2)]
+        w2_scales = [sbuf(f"w2_scales{duo}", [P, 2, P], U8) for duo in range(2)]
 
-        def round_w2(half, duo):
-            w2_dealt[half, duo] = sbuf(f"w2_dealt{half}{duo}", [P, 2, HALF, PACK], BF16)
-            src = w2_raw[half][:].rearrange("p j (m t) -> p m j t", t=PACK)[:, :, :, 2 * duo : 2 * duo + 2]
-            nc.vector.tensor_copy(w2_dealt[half, duo][:].rearrange("p t m j -> p m j t"), src)
+        def round_w2(part, duo):
+            lo, hi = w2_parts[part]
+            src = w2_raw[part][:].rearrange("p j (m t) -> p m j t", t=PACK)[:, :, :, 2 * duo : 2 * duo + 2]
+            nc.vector.tensor_copy(w2_dealt[duo][:].rearrange("p t m j -> p m j t")[:, lo:hi], src)
 
-        def quantize_w2(half, t):
-            cols = slice(half * HALF, (half + 1) * HALF)
-            quantize(w2_codes[t][:, cols], w2_scales[t][:, cols], w2_dealt[half, t // 2][:, t % 2].rearrange("p m j -> p (m j)"))
+        def quantize_w2(duo):
+            quantize(
+                w2_codes[duo][:].rearrange("p t m -> p (t m)"),
+                w2_scales[duo][:].rearrange("p t m -> p (t m)"),
+                w2_dealt[duo][:].rearrange("p t m j -> p (t m j)"),
+            )
 
         h_bf = sbuf("h_bf", [P, S, PACK], BF16)
         h_codes = {}
@@ -150,21 +155,21 @@ def tile_picked_zgrn_relu_po_kernel(tc, x_words, x_scales, w1, w2, offs, out_0, 
         y_rows = out_0.rearrange("(p t) n -> p t n", t=PACK)
         word_rows = out_1[0].rearrange("p n t -> p (n t)").bitcast(I32)
 
-        def gate_and_result(duo, first, count, width, bank):
-            logits = psum.tile([P, 2, count * CHUNK], F32, name=f"logits{duo}{first}", tag=bank)
+        def gate_and_result(t0, tiles, first, count, width, bank):
+            logits = psum.tile([P, tiles, count * CHUNK], F32, name=f"logits{t0}{first}", tag=bank)
             for lo in range(0, count, width):
-                for i in range(2):
-                    t = 2 * duo + i
+                for i in range(tiles):
+                    t = t0 + i
                     product(
                         logits[:, i, lo * CHUNK : (lo + width) * CHUNK],
-                        w2_codes[t][:],
-                        w2_scales[t][:],
+                        w2_codes[t // 2][:, t % 2, :],
+                        w2_scales[t // 2][:, t % 2, :],
                         h_codes[first + lo, width],
                         h_scales[first + lo, width],
                     )
-            gate = sbuf(f"gate{duo}{first}", [P, 2, count * CHUNK], F32)
+            gate = sbuf(f"gate{t0}{first}", [P, tiles, count * CHUNK], F32)
             nc.scalar.activation(gate[:], logits[:], ACT.Sigmoid)
-            ts = slice(2 * duo, 2 * duo + 2)
+            ts = slice(t0, t0 + tiles)
             for i in range(count):
                 c = first + i
                 nc.vector.scalar_tensor_tensor(
@@ -180,10 +185,10 @@ def tile_picked_zgrn_relu_po_kernel(tc, x_words, x_scales, w1, w2, offs, out_0, 
             ts = slice(2 * duo, 2 * duo + 2)
             nc.sync.dma_start(out=y_rows[:, ts, g * PAIR : (g + 1) * PAIR], in_=y[g][:, ts, :])
 
-        def round_result(first, count, engine):
-            lo = (first % 2) * CHUNK
-            dst = y_bf[:, first * CHUNK : (first + count) * CHUNK, :]
-            src = y[first // 2][:, :, lo : lo + count * CHUNK]
+        def round_result(lo, hi, engine):
+            g = lo // PAIR
+            dst = y_bf[:, lo:hi, :]
+            src = y[g][:, :, lo - g * PAIR : hi - g * PAIR]
             if engine == "gpsimd":
                 nc.gpsimd.tensor_scalar(dst, src.rearrange("p t n -> p n t"), 1.0, 0.0, ALU.mult, ALU.add)
             else:
@@ -201,36 +206,35 @@ def tile_picked_zgrn_relu_po_kernel(tc, x_words, x_scales, w1, w2, offs, out_0, 
             round_hidden(c)
         round_w2(0, 0)
         round_w2(0, 1)
-        for t in range(PACK):
-            quantize_w2(0, t)
-        quantize_hidden(0, 1, "w2_raw0")
         round_w2(1, 0)
         round_w2(1, 1)
-        quantize_w2(1, 0)
-        quantize_w2(1, 1)
-        quantize_hidden(1, 1, "w2_raw1")
-        quantize_w2(1, 2)
-        quantize_w2(1, 3)
-        quantize_hidden(2, 2, "w2_dealt10")
-        gate_and_result(0, 0, 1, 1, "logits_a")
-        gate_and_result(0, 1, 1, 1, "logits_b")
+        quantize_w2(0)
+        quantize_hidden(0, 1, "w2_raw1")
+        quantize_hidden(1, 1, "w2_dealt0")
+        quantize_w2(1)
+        quantize_hidden(2, 2, "w2_dealt1")
+        gate_and_result(0, 2, 0, 1, 1, "logits_a")
+        gate_and_result(0, 2, 1, 1, 1, "logits_b")
         store_result(0, 0)
-        gate_and_result(1, 0, 2, 1, "logits_c")
+        gate_and_result(2, 2, 0, 1, 1, "logits_c")
+        gate_and_result(2, 2, 1, 1, 1, "logits_d")
         store_result(1, 0)
-        gate_and_result(0, 2, 2, 2, "logits_d")
+        gate_and_result(0, 2, 2, 1, 1, "logits_a")
+        gate_and_result(0, 2, 3, 1, 1, "logits_b")
         store_result(0, 1)
-        gate_and_result(1, 2, 1, 1, "logits_a")
-        gate_and_result(1, 3, 1, 1, "logits_b")
+        gate_and_result(2, 2, 2, 1, 1, "logits_c")
+        gate_and_result(2, 2, 3, 1, 1, "logits_d")
         store_result(1, 1)
-        round_result(0, 1, "gpsimd")
-        round_result(1, 1, "scalar")
-        round_result(2, 1, "scalar")
+        round_result(0, CHUNK, "gpsimd")
+        round_result(CHUNK, CHUNK + HALF, "gpsimd")
+        round_result(CHUNK + HALF, PAIR, "scalar")
+        round_result(PAIR, PAIR + CHUNK, "scalar")
         quantize_result(0, 1)
-        round_result(3, 1, "vector")
         quantize_result(1, 1)
         store_codes(0)
-        quantize_result(3, 1)
+        round_result(PAIR + CHUNK, S, "vector")
         quantize_result(2, 1)
+        quantize_result(3, 1)
         store_codes(1)
         for q in range(4):
             queue = nc.scalar if q % 2 == 0 else nc.sync

@@ -226,13 +226,12 @@ def tile_picked_zgrn_relu_po_kernel(tc, x_words, x_scales, w1, w2, offs, out_0, 
         gate_and_result(2, 2, 3, 1, 1, "logits_d")
         store_result(1, 1)
         round_result(0, CHUNK, "gpsimd")
-        round_result(CHUNK, CHUNK + HALF, "gpsimd")
-        round_result(CHUNK + HALF, PAIR, "scalar")
-        round_result(PAIR, PAIR + CHUNK, "scalar")
+        round_result(CHUNK, PAIR, "scalar")
+        round_result(PAIR, PAIR + CHUNK, "vector")
         quantize_result(0, 1)
+        round_result(PAIR + CHUNK, S, "vector")
         quantize_result(1, 1)
         store_codes(0)
-        round_result(PAIR + CHUNK, S, "vector")
         quantize_result(2, 1)
         quantize_result(3, 1)
         store_codes(1)

@@ -22,7 +22,7 @@ CHUNK = 128
 CHUNKS = S // CHUNK
 PAIR = 2 * CHUNK
 W1_ON_SCALAR = 96
-W2_EARLY = 80
+W2_EARLY = 88
 
 
 def tile_picked_zgrn_relu_po_kernel(tc, x_words, x_scales, w1, w2, offs, out_0, out_1, out_2):
@@ -206,11 +206,11 @@ def tile_picked_zgrn_relu_po_kernel(tc, x_words, x_scales, w1, w2, offs, out_0, 
             round_hidden(c)
         round_w2(0, 0)
         round_w2(0, 1)
+        quantize_hidden(0, 1, "w2_raw0")
         round_w2(1, 0)
         round_w2(1, 1)
         quantize_w2(0)
-        quantize_hidden(0, 1, "w2_raw1")
-        quantize_hidden(1, 1, "w2_dealt0")
+        quantize_hidden(1, 1, "w2_raw1")
         quantize_w2(1)
         quantize_hidden(2, 2, "w2_dealt1")
         gate_and_result(0, 2, 0, 1, 1, "logits_a")
@@ -228,12 +228,11 @@ def tile_picked_zgrn_relu_po_kernel(tc, x_words, x_scales, w1, w2, offs, out_0, 
         round_result(0, CHUNK, "gpsimd")
         round_result(CHUNK, PAIR, "scalar")
         round_result(PAIR, PAIR + CHUNK, "vector")
-        quantize_result(0, 1)
-        round_result(PAIR + CHUNK, S, "vector")
-        quantize_result(1, 1)
+        round_result(PAIR + CHUNK, S - HALF, "vector")
+        round_result(S - HALF, S, "scalar")
+        quantize_result(0, 2)
         store_codes(0)
-        quantize_result(2, 1)
-        quantize_result(3, 1)
+        quantize_result(2, 2)
         store_codes(1)
         for q in range(4):
             queue = nc.scalar if q % 2 == 0 else nc.sync

@@ -21,7 +21,6 @@ HALF = 64
 CHUNK = 128
 CHUNKS = S // CHUNK
 PAIR = 2 * CHUNK
-W1_ON_SCALAR = 96
 W2_EARLY = 88
 
 
@@ -102,8 +101,7 @@ def tile_picked_zgrn_relu_po_kernel(tc, x_words, x_scales, w1, w2, offs, out_0, 
             nc.vector.tensor_copy(x_codes[:, lo:hi], word_table[:].indirect(offsets[:, lo // 16 : hi // 16]))
 
         round_w1(0, 0, P, "vector")
-        round_w1(1, 0, W1_ON_SCALAR, "scalar")
-        round_w1(1, W1_ON_SCALAR, P, "vector")
+        round_w1(1, 0, P, "scalar")
         quantize_w1(0)
         gather_words(0, CHUNK)
         quantize_w1(1)

@@ -84,9 +84,9 @@ def tile_picked_zgrn_relu_po_kernel(tc, x_words, x_scales, w1, w2, offs, out_0, 
         w1_codes = [sbuf(f"w1_codes{duo}", [P, 2, P], U32) for duo in range(2)]
         w1_scales = [sbuf(f"w1_scales{duo}", [P, 2, P], U8) for duo in range(2)]
 
-        def round_w1(duo, lo, hi, engine):
-            src = w1_raw[:].rearrange("p j (m t) -> p m j t", t=PACK)[:, lo:hi, :, 2 * duo : 2 * duo + 2]
-            round_copy(engine, w1_dealt[duo][:].rearrange("p t m j -> p m j t")[:, lo:hi], src)
+        def round_w1(duo, rows, engine):
+            src = w1_raw[:].rearrange("p j (m t) -> p m j t", t=PACK)[:, :, rows, 2 * duo : 2 * duo + 2]
+            round_copy(engine, w1_dealt[duo][:].rearrange("p t m j -> p m j t")[:, :, rows], src)
 
         def quantize_w1(duo):
             quantize(
@@ -100,8 +100,9 @@ def tile_picked_zgrn_relu_po_kernel(tc, x_words, x_scales, w1, w2, offs, out_0, 
         def gather_words(lo, hi):
             nc.vector.tensor_copy(x_codes[:, lo:hi], word_table[:].indirect(offsets[:, lo // 16 : hi // 16]))
 
-        round_w1(0, 0, P, "vector")
-        round_w1(1, 0, P, "scalar")
+        round_w1(0, slice(0, 2), "scalar")
+        round_w1(0, slice(2, 4), "vector")
+        round_w1(1, slice(0, 4), "scalar")
         quantize_w1(0)
         gather_words(0, CHUNK)
         quantize_w1(1)
@@ -114,20 +115,20 @@ def tile_picked_zgrn_relu_po_kernel(tc, x_words, x_scales, w1, w2, offs, out_0, 
             for t in range(PACK):
                 product(pre[c][:, t, :], w1_codes[t // 2][:, t % 2, :], w1_scales[t // 2][:, t % 2, :], x_codes[:, cols], x_bytes[:, cols])
 
-        w2_dealt = [sbuf(f"w2_dealt{duo}", [P, 2, P, PACK], BF16) for duo in range(2)]
+        w2_dealt = sbuf("w2_dealt", [P, PACK, P, PACK], BF16)
         w2_codes = [sbuf(f"w2_codes{duo}", [P, 2, P], U32) for duo in range(2)]
         w2_scales = [sbuf(f"w2_scales{duo}", [P, 2, P], U8) for duo in range(2)]
 
-        def round_w2(part, duo):
+        def round_w2(part, tiles):
             lo, hi = w2_parts[part]
-            src = w2_raw[part][:].rearrange("p j (m t) -> p m j t", t=PACK)[:, :, :, 2 * duo : 2 * duo + 2]
-            nc.vector.tensor_copy(w2_dealt[duo][:].rearrange("p t m j -> p m j t")[:, lo:hi], src)
+            src = w2_raw[part][:].rearrange("p j (m t) -> p m j t", t=PACK)[:, :, :, tiles]
+            nc.vector.tensor_copy(w2_dealt[:].rearrange("p t m j -> p m j t")[:, lo:hi, :, tiles], src)
 
         def quantize_w2(duo):
             quantize(
                 w2_codes[duo][:].rearrange("p t m -> p (t m)"),
                 w2_scales[duo][:].rearrange("p t m -> p (t m)"),
-                w2_dealt[duo][:].rearrange("p t m j -> p (t m j)"),
+                w2_dealt[:, 2 * duo : 2 * duo + 2].rearrange("p t m j -> p (t m j)"),
             )
 
         h_bf = sbuf("h_bf", [P, S, PACK], BF16)
@@ -202,15 +203,14 @@ def tile_picked_zgrn_relu_po_kernel(tc, x_words, x_scales, w1, w2, offs, out_0, 
 
         for c in range(CHUNKS):
             round_hidden(c)
-        round_w2(0, 0)
-        round_w2(0, 1)
+        round_w2(0, slice(0, 4))
         quantize_hidden(0, 1, "w2_raw0")
-        round_w2(1, 0)
-        round_w2(1, 1)
+        round_w2(1, slice(0, 2))
+        round_w2(1, slice(2, 4))
         quantize_w2(0)
         quantize_hidden(1, 1, "w2_raw1")
         quantize_w2(1)
-        quantize_hidden(2, 2, "w2_dealt1")
+        quantize_hidden(2, 2, "w2_dealt")
         gate_and_result(0, 2, 0, 1, 1, "logits_a")
         gate_and_result(0, 2, 1, 1, 1, "logits_b")
         store_result(0, 0)

@@ -17,11 +17,13 @@ ALU = mybir.AluOpType
 
 P = 128
 PACK = 4
-HALF = 64
 CHUNK = 128
 CHUNKS = S // CHUNK
 PAIR = 2 * CHUNK
 W2_EARLY = 88
+LAST_ON_SCALAR = 64
+
+JOINT = ["h1", "w0", "w1", "w2", "w3", "h2", "h3"]
 
 
 def tile_picked_zgrn_relu_po_kernel(tc, x_words, x_scales, w1, w2, offs, out_0, out_1, out_2):
@@ -33,76 +35,57 @@ def tile_picked_zgrn_relu_po_kernel(tc, x_words, x_scales, w1, w2, offs, out_0, 
         def sbuf(name, shape, dtype, tag=None):
             return keep.tile(shape, dtype, name=name, tag=tag or name, align_bytes=64)
 
+        def quantize(codes, scales, values):
+            nc.vector.quantize_mx(out=codes.bitcast(FP8X4), scales=scales, in_=values)
+
+        def product(out, w_codes, w_scales, a_codes, a_scales):
+            nc.tensor.matmul_mx(out=out, lhsT=w_codes.bitcast(FP8X4), lhsT_scale=w_scales, rhs=a_codes.bitcast(FP8X4), rhs_scale=a_scales, start=True, stop=True)
+
         offsets = keep.tile([P, S // 16], U16, name="offsets")
         word_table = sbuf("word_table", [P, T], U32)
         scale_table = sbuf("scale_table", [P, T], U8)
         w1_raw = sbuf("w1_raw", [P, PACK, H], F32)
         w1_rows = w1.rearrange("(p j) c -> p j c", j=PACK)
         w2_rows = w2.rearrange("(p j) c -> p j c", j=PACK)
-        nc.vector.memset(scale_table[:].bitcast(I32), 0)
+        nc.gpsimd.memset(scale_table[:].bitcast(I32), 0)
         nc.sync.dma_start(out=w1_raw[:, 0:2, :], in_=w1_rows[:, 0:2, :])
         nc.sync.dma_start(offsets[:], offs)
         for q in range(4):
             nc.sync.dma_start(out=scale_table[32 * q : 32 * q + 4, :].bitcast(I32), in_=x_scales[0, 4 * q : 4 * q + 4, :].bitcast(I32))
         nc.sync.dma_start(out=w1_raw[:, 2:4, :], in_=w1_rows[:, 2:4, :])
         nc.sync.dma_start(out=word_table[:].bitcast(I32), in_=x_words[0].rearrange("p n t -> p (n t)").bitcast(I32))
-        w2_raw = []
         w2_parts = [(0, W2_EARLY), (W2_EARLY, P)]
+        w2_raw = []
         for part, (lo, hi) in enumerate(w2_parts):
             w2_raw.append(sbuf(f"w2_raw{part}", [P, PACK, (hi - lo) * PACK], F32))
             nc.sync.dma_start(out=w2_raw[part][:], in_=w2_rows[:, :, lo * PACK : hi * PACK])
 
         warm_in = sbuf("warm_in", [P, 1], F32)
         warm_out = sbuf("warm_out", [P, 1], F32)
-        nc.vector.memset(warm_in[:], 0.0)
+        nc.gpsimd.memset(warm_in[:], 0.0)
         nc.scalar.activation(warm_out[:], warm_in[:], ACT.Sigmoid)
 
         x_bytes = sbuf("x_bytes", [P, S], U8)
+        x_codes = sbuf("x_codes", [P, S], U32)
         nc.vector.tensor_copy(x_bytes[:], scale_table[:].indirect(offsets[:]))
 
-        def round_copy(engine, dst, src):
-            if engine == "scalar":
-                nc.scalar.copy(dst, src)
-            else:
-                nc.vector.tensor_copy(dst, src)
-
-        def quantize(codes, scales, values):
-            nc.vector.quantize_mx(out=codes.bitcast(FP8X4), scales=scales, in_=values)
-
-        def product(out, w_codes, w_scales, a_codes, a_scales):
-            nc.tensor.matmul_mx(
-                out=out,
-                lhsT=w_codes.bitcast(FP8X4),
-                lhsT_scale=w_scales,
-                rhs=a_codes.bitcast(FP8X4),
-                rhs_scale=a_scales,
-                start=True,
-                stop=True,
-            )
-
         w1_dealt = [sbuf(f"w1_dealt{duo}", [P, 2, P, PACK], BF16) for duo in range(2)]
-        w1_codes = [sbuf(f"w1_codes{duo}", [P, 2, P], U32) for duo in range(2)]
-        w1_scales = [sbuf(f"w1_scales{duo}", [P, 2, P], U8) for duo in range(2)]
+        w1_codes = [sbuf(f"w1_codes{duo}", [P, 2 * P], U32) for duo in range(2)]
+        w1_scales = [sbuf(f"w1_scales{duo}", [P, 2 * P], U8) for duo in range(2)]
 
-        def round_w1(duo, rows, engine):
+        def w1_views(duo, rows):
             src = w1_raw[:].rearrange("p j (m t) -> p m j t", t=PACK)[:, :, rows, 2 * duo : 2 * duo + 2]
-            round_copy(engine, w1_dealt[duo][:].rearrange("p t m j -> p m j t")[:, :, rows], src)
+            return w1_dealt[duo][:].rearrange("p t m j -> p m j t")[:, :, rows], src
 
         def quantize_w1(duo):
-            quantize(
-                w1_codes[duo][:].rearrange("p t m -> p (t m)"),
-                w1_scales[duo][:].rearrange("p t m -> p (t m)"),
-                w1_dealt[duo][:].rearrange("p t m j -> p (t m j)"),
-            )
-
-        x_codes = sbuf("x_codes", [P, S], U32)
+            quantize(w1_codes[duo][:], w1_scales[duo][:], w1_dealt[duo][:].rearrange("p t m j -> p (t m j)"))
 
         def gather_words(lo, hi):
             nc.vector.tensor_copy(x_codes[:, lo:hi], word_table[:].indirect(offsets[:, lo // 16 : hi // 16]))
 
-        round_w1(0, slice(0, 2), "scalar")
-        round_w1(0, slice(2, 4), "vector")
-        round_w1(1, slice(0, 4), "scalar")
+        nc.scalar.copy(*w1_views(0, slice(0, 2)))
+        nc.vector.tensor_copy(*w1_views(0, slice(2, 4)))
+        nc.scalar.copy(*w1_views(1, slice(0, 4)))
         quantize_w1(0)
         gather_words(0, CHUNK)
         quantize_w1(1)
@@ -113,125 +96,90 @@ def tile_picked_zgrn_relu_po_kernel(tc, x_words, x_scales, w1, w2, offs, out_0, 
         for c in range(CHUNKS):
             cols = slice(c * CHUNK, (c + 1) * CHUNK)
             for t in range(PACK):
-                product(pre[c][:, t, :], w1_codes[t // 2][:, t % 2, :], w1_scales[t // 2][:, t % 2, :], x_codes[:, cols], x_bytes[:, cols])
+                wcols = slice((t % 2) * P, (t % 2 + 1) * P)
+                product(pre[c][:, t, :], w1_codes[t // 2][:, wcols], w1_scales[t // 2][:, wcols], x_codes[:, cols], x_bytes[:, cols])
 
-        w2_dealt = sbuf("w2_dealt", [P, PACK, P, PACK], BF16)
-        w2_codes = [sbuf(f"w2_codes{duo}", [P, 2, P], U32) for duo in range(2)]
-        w2_scales = [sbuf(f"w2_scales{duo}", [P, 2, P], U8) for duo in range(2)]
+        joint_bf = sbuf("joint_bf", [P, len(JOINT) * P * PACK], BF16)
+        joint_codes = sbuf("joint_codes", [P, len(JOINT) * P], U32)
+        joint_scales = sbuf("joint_scales", [P, len(JOINT) * P], U8)
+        h0_bf = sbuf("h0_bf", [P, CHUNK * PACK], BF16)
+
+        def block(name, count=1, width=P):
+            at = JOINT.index(name)
+            return slice(at * width, (at + count) * width)
+
+        def round_hidden(c):
+            dst = h0_bf[:] if c == 0 else joint_bf[:, block(f"h{c}", 1, P * PACK)]
+            nc.scalar.activation(dst.rearrange("p (n t) -> p n t", t=PACK), pre[c][:].rearrange("p t n -> p n t"), ACT.Relu)
 
         def round_w2(part, tiles):
             lo, hi = w2_parts[part]
-            src = w2_raw[part][:].rearrange("p j (m t) -> p m j t", t=PACK)[:, :, :, tiles]
-            nc.vector.tensor_copy(w2_dealt[:].rearrange("p t m j -> p m j t")[:, lo:hi, :, tiles], src)
+            dst = joint_bf[:, block("w0", PACK, P * PACK)].rearrange("p (t m j) -> p m j t", t=PACK, j=PACK)
+            src = w2_raw[part][:].rearrange("p j (m t) -> p m j t", t=PACK)
+            nc.vector.tensor_copy(dst[:, lo:hi, :, tiles], src[:, :, :, tiles])
 
-        def quantize_w2(duo):
-            quantize(
-                w2_codes[duo][:].rearrange("p t m -> p (t m)"),
-                w2_scales[duo][:].rearrange("p t m -> p (t m)"),
-                w2_dealt[:, 2 * duo : 2 * duo + 2].rearrange("p t m j -> p (t m j)"),
-            )
-
-        h_bf = sbuf("h_bf", [P, S, PACK], BF16)
-        h_codes = {}
-        h_scales = {}
-        y = [sbuf(f"y{g}", [P, PACK, PAIR], F32) for g in range(2)]
-        y_bf = sbuf("y_bf", [P, S, PACK], BF16)
-        y_codes = sbuf("y_codes", [P, S], U32)
-        y_scales = sbuf("y_scales", [P, S], U8)
-
-        def round_hidden(c):
-            nc.scalar.activation(h_bf[:, c * CHUNK : (c + 1) * CHUNK, :], pre[c][:].rearrange("p t n -> p n t"), ACT.Relu)
-
-        def quantize_hidden(first, count, slot):
-            codes = sbuf(f"h_codes{first}", [P, count * CHUNK], U32, tag=slot)
-            scales = sbuf(f"h_scales{first}", [P, count * CHUNK], U8)
-            quantize(codes[:], scales[:], h_bf[:, first * CHUNK : (first + count) * CHUNK, :].rearrange("p n t -> p (n t)"))
-            for n in range(1, count + 1):
-                for i in range(count - n + 1):
-                    h_codes[first + i, n] = codes[:, i * CHUNK : (i + n) * CHUNK]
-                    h_scales[first + i, n] = scales[:, i * CHUNK : (i + n) * CHUNK]
-
-        y_rows = out_0.rearrange("(p t) n -> p t n", t=PACK)
-        word_rows = out_1[0].rearrange("p n t -> p (n t)").bitcast(I32)
-
-        def gate_and_result(t0, tiles, first, count, width, bank):
-            logits = psum.tile([P, tiles, count * CHUNK], F32, name=f"logits{t0}{first}", tag=bank)
-            for lo in range(0, count, width):
-                for i in range(tiles):
-                    t = t0 + i
-                    product(
-                        logits[:, i, lo * CHUNK : (lo + width) * CHUNK],
-                        w2_codes[t // 2][:, t % 2, :],
-                        w2_scales[t // 2][:, t % 2, :],
-                        h_codes[first + lo, width],
-                        h_scales[first + lo, width],
-                    )
-            gate = sbuf(f"gate{t0}{first}", [P, tiles, count * CHUNK], F32)
-            nc.scalar.activation(gate[:], logits[:], ACT.Sigmoid)
-            ts = slice(t0, t0 + tiles)
-            for i in range(count):
-                c = first + i
-                nc.vector.scalar_tensor_tensor(
-                    y[c // 2][:, ts, (c % 2) * CHUNK : (c % 2 + 1) * CHUNK],
-                    pre[c][:, ts, :],
-                    0.0,
-                    gate[:, :, i * CHUNK : (i + 1) * CHUNK],
-                    ALU.max,
-                    ALU.mult,
-                )
-
-        def store_result(duo, g):
-            ts = slice(2 * duo, 2 * duo + 2)
-            nc.sync.dma_start(out=y_rows[:, ts, g * PAIR : (g + 1) * PAIR], in_=y[g][:, ts, :])
-
-        def round_result(lo, hi, engine):
-            g = lo // PAIR
-            dst = y_bf[:, lo:hi, :]
-            src = y[g][:, :, lo - g * PAIR : hi - g * PAIR]
-            if engine == "gpsimd":
-                nc.gpsimd.tensor_scalar(dst, src.rearrange("p t n -> p n t"), 1.0, 0.0, ALU.mult, ALU.add)
-            else:
-                round_copy(engine, dst.rearrange("p (g i) t -> p g t i", i=4), src.rearrange("p t (g i) -> p g t i", i=4))
-
-        def quantize_result(first, count):
-            cols = slice(first * CHUNK, (first + count) * CHUNK)
-            quantize(y_codes[:, cols], y_scales[:, cols], y_bf[:, cols, :].rearrange("p n t -> p (n t)"))
-
-        def store_codes(g):
-            cols = slice(g * PAIR, (g + 1) * PAIR)
-            nc.sync.dma_start(out=word_rows[:, cols], in_=y_codes[:, cols].bitcast(I32))
+        def quantize_joint(first, count):
+            quantize(joint_codes[:, block(first, count)], joint_scales[:, block(first, count)], joint_bf[:, block(first, count, P * PACK)])
 
         for c in range(CHUNKS):
             round_hidden(c)
         round_w2(0, slice(0, 4))
-        quantize_hidden(0, 1, "w2_raw0")
+        h0_codes = sbuf("h0_codes", [P, CHUNK], U32, tag="w2_raw0")
+        h0_scales = sbuf("h0_scales", [P, CHUNK], U8)
+        quantize(h0_codes[:], h0_scales[:], h0_bf[:])
         round_w2(1, slice(0, 2))
         round_w2(1, slice(2, 4))
-        quantize_w2(0)
-        quantize_hidden(1, 1, "w2_raw1")
-        quantize_w2(1)
-        quantize_hidden(2, 2, "w2_dealt")
-        gate_and_result(0, 2, 0, 1, 1, "logits_a")
-        gate_and_result(0, 2, 1, 1, 1, "logits_b")
-        store_result(0, 0)
-        gate_and_result(2, 2, 0, 1, 1, "logits_c")
-        gate_and_result(2, 2, 1, 1, 1, "logits_d")
-        store_result(1, 0)
-        gate_and_result(0, 2, 2, 1, 1, "logits_a")
-        gate_and_result(0, 2, 3, 1, 1, "logits_b")
-        store_result(0, 1)
-        gate_and_result(2, 2, 2, 1, 1, "logits_c")
-        gate_and_result(2, 2, 3, 1, 1, "logits_d")
-        store_result(1, 1)
-        round_result(0, CHUNK, "gpsimd")
-        round_result(CHUNK, PAIR, "scalar")
-        round_result(PAIR, PAIR + CHUNK, "vector")
-        round_result(PAIR + CHUNK, S - HALF, "vector")
-        round_result(S - HALF, S, "scalar")
-        quantize_result(0, 2)
-        store_codes(0)
-        quantize_result(2, 2)
-        store_codes(1)
+        quantize_joint("h1", 3)
+        quantize_joint("w2", 2)
+        quantize_joint("h2", 2)
+
+        y = [sbuf(f"y{g}", [P, PACK, PAIR], F32) for g in range(2)]
+        y_bf = sbuf("y_bf", [P, S, PACK], BF16)
+        y_codes = sbuf("y_codes", [P, S], U32)
+        y_scales = sbuf("y_scales", [P, S], U8)
+        y_rows = out_0.rearrange("(p t) n -> p t n", t=PACK)
+        word_rows = out_1[0].rearrange("p n t -> p (n t)").bitcast(I32)
+
+        def gate_and_result(duo, c, bank):
+            logits = psum.tile([P, 2, CHUNK], F32, name=f"logits{duo}{c}", tag=bank)
+            for i in range(2):
+                w = block(f"w{2 * duo + i}")
+                if c == 0:
+                    product(logits[:, i, :], joint_codes[:, w], joint_scales[:, w], h0_codes[:], h0_scales[:])
+                else:
+                    a = block(f"h{c}")
+                    product(logits[:, i, :], joint_codes[:, w], joint_scales[:, w], joint_codes[:, a], joint_scales[:, a])
+            gate = sbuf(f"gate{duo}{c}", [P, 2, CHUNK], F32)
+            nc.scalar.activation(gate[:], logits[:], ACT.Sigmoid)
+            ts = slice(2 * duo, 2 * duo + 2)
+            nc.vector.scalar_tensor_tensor(y[c // 2][:, ts, (c % 2) * CHUNK : (c % 2 + 1) * CHUNK], pre[c][:, ts, :], 0.0, gate[:], ALU.max, ALU.mult)
+
+        banks = ["logits_a", "logits_b", "logits_c", "logits_d"]
+        for g in range(2):
+            for duo in range(2):
+                for i in range(2):
+                    gate_and_result(duo, 2 * g + i, banks[2 * duo + i])
+                ts = slice(2 * duo, 2 * duo + 2)
+                nc.sync.dma_start(out=y_rows[:, ts, g * PAIR : (g + 1) * PAIR], in_=y[g][:, ts, :])
+
+        def result_views(lo, hi):
+            g = lo // PAIR
+            return y_bf[:, lo:hi, :], y[g][:, :, lo - g * PAIR : hi - g * PAIR]
+
+        def by_fours(lo, hi):
+            dst, src = result_views(lo, hi)
+            return dst.rearrange("p (g i) t -> p g t i", i=4), src.rearrange("p t (g i) -> p g t i", i=4)
+
+        dst, src = result_views(0, CHUNK)
+        nc.gpsimd.tensor_scalar(dst, src.rearrange("p t n -> p n t"), 1.0, 0.0, ALU.mult, ALU.add)
+        nc.scalar.copy(*by_fours(CHUNK, PAIR))
+        nc.vector.tensor_copy(*by_fours(PAIR, PAIR + CHUNK))
+        nc.vector.tensor_copy(*by_fours(PAIR + CHUNK, S - LAST_ON_SCALAR))
+        nc.scalar.copy(*by_fours(S - LAST_ON_SCALAR, S))
+        for g in range(2):
+            cols = slice(g * PAIR, (g + 1) * PAIR)
+            quantize(y_codes[:, cols], y_scales[:, cols], y_bf[:, cols, :].rearrange("p n t -> p (n t)"))
+            nc.sync.dma_start(out=word_rows[:, cols], in_=y_codes[:, cols].bitcast(I32))
         for q in range(4):
             queue = nc.scalar if q % 2 == 0 else nc.sync
             queue.dma_start(out=out_2[0, 4 * q : 4 * q + 4, :].bitcast(I32), in_=y_scales[32 * q : 32 * q + 4, :].bitcast(I32))

@@ -20,10 +20,11 @@ PACK = 4
 CHUNK = 128
 CHUNKS = S // CHUNK
 PAIR = 2 * CHUNK
+W2_ON_SCALAR = 32
 W2_EARLY = 88
 LAST_ON_SCALAR = 64
 
-JOINT = ["h1", "w0", "w1", "w2", "w3", "h2", "h3"]
+JOINT = ["w0", "w1", "w2", "w3"]
 
 
 def tile_picked_zgrn_relu_po_kernel(tc, x_words, x_scales, w1, w2, offs, out_0, out_1, out_2):
@@ -47,14 +48,14 @@ def tile_picked_zgrn_relu_po_kernel(tc, x_words, x_scales, w1, w2, offs, out_0, 
         w1_raw = sbuf("w1_raw", [P, PACK, H], F32)
         w1_rows = w1.rearrange("(p j) c -> p j c", j=PACK)
         w2_rows = w2.rearrange("(p j) c -> p j c", j=PACK)
-        nc.gpsimd.memset(scale_table[:].bitcast(I32), 0)
+        nc.vector.memset(scale_table[:].bitcast(I32), 0)
         nc.sync.dma_start(out=w1_raw[:, 0:2, :], in_=w1_rows[:, 0:2, :])
         nc.sync.dma_start(offsets[:], offs)
         for q in range(4):
             nc.sync.dma_start(out=scale_table[32 * q : 32 * q + 4, :].bitcast(I32), in_=x_scales[0, 4 * q : 4 * q + 4, :].bitcast(I32))
         nc.sync.dma_start(out=w1_raw[:, 2:4, :], in_=w1_rows[:, 2:4, :])
         nc.sync.dma_start(out=word_table[:].bitcast(I32), in_=x_words[0].rearrange("p n t -> p (n t)").bitcast(I32))
-        w2_parts = [(0, W2_EARLY), (W2_EARLY, P)]
+        w2_parts = [(0, W2_ON_SCALAR), (W2_ON_SCALAR, W2_EARLY), (W2_EARLY, P)]
         w2_raw = []
         for part, (lo, hi) in enumerate(w2_parts):
             w2_raw.append(sbuf(f"w2_raw{part}", [P, PACK, (hi - lo) * PACK], F32))
@@ -62,7 +63,7 @@ def tile_picked_zgrn_relu_po_kernel(tc, x_words, x_scales, w1, w2, offs, out_0, 
 
         warm_in = sbuf("warm_in", [P, 1], F32)
         warm_out = sbuf("warm_out", [P, 1], F32)
-        nc.gpsimd.memset(warm_in[:], 0.0)
+        nc.vector.memset(warm_in[:], 0.0)
         nc.scalar.activation(warm_out[:], warm_in[:], ACT.Sigmoid)
 
         x_bytes = sbuf("x_bytes", [P, S], U8)
@@ -100,38 +101,48 @@ def tile_picked_zgrn_relu_po_kernel(tc, x_words, x_scales, w1, w2, offs, out_0, 
                 product(pre[c][:, t, :], w1_codes[t // 2][:, wcols], w1_scales[t // 2][:, wcols], x_codes[:, cols], x_bytes[:, cols])
 
         joint_bf = sbuf("joint_bf", [P, len(JOINT) * P * PACK], BF16)
-        joint_codes = sbuf("joint_codes", [P, len(JOINT) * P], U32)
-        joint_scales = sbuf("joint_scales", [P, len(JOINT) * P], U8)
-        h0_bf = sbuf("h0_bf", [P, CHUNK * PACK], BF16)
+        operand = {}
+        h_bf = sbuf("h_bf", [P, S * PACK], BF16, tag="w2_raw0")
 
         def block(name, count=1, width=P):
             at = JOINT.index(name)
             return slice(at * width, (at + count) * width)
 
         def round_hidden(c):
-            dst = h0_bf[:] if c == 0 else joint_bf[:, block(f"h{c}", 1, P * PACK)]
+            dst = h_bf[:, c * CHUNK * PACK : (c + 1) * CHUNK * PACK]
             nc.scalar.activation(dst.rearrange("p (n t) -> p n t", t=PACK), pre[c][:].rearrange("p t n -> p n t"), ACT.Relu)
 
-        def round_w2(part, tiles):
+        def quantize_hidden(first, count, slot):
+            codes = sbuf(f"h_codes{first}", [P, count * CHUNK], U32, tag=slot)
+            scales = sbuf(f"h_scales{first}", [P, count * CHUNK], U8)
+            quantize(codes[:], scales[:], h_bf[:, first * CHUNK * PACK : (first + count) * CHUNK * PACK])
+            for i in range(count):
+                operand[f"h{first + i}"] = (codes[:, i * CHUNK : (i + 1) * CHUNK], scales[:, i * CHUNK : (i + 1) * CHUNK])
+
+        def round_w2(copy, part, tiles):
             lo, hi = w2_parts[part]
             dst = joint_bf[:, block("w0", PACK, P * PACK)].rearrange("p (t m j) -> p m j t", t=PACK, j=PACK)
             src = w2_raw[part][:].rearrange("p j (m t) -> p m j t", t=PACK)
-            nc.vector.tensor_copy(dst[:, lo:hi, :, tiles], src[:, :, :, tiles])
+            copy(dst[:, lo:hi, :, tiles], src[:, :, :, tiles])
 
         def quantize_joint(first, count):
-            quantize(joint_codes[:, block(first, count)], joint_scales[:, block(first, count)], joint_bf[:, block(first, count, P * PACK)])
+            codes = sbuf(f"codes_{first}", [P, count * P], U32)
+            scales = sbuf(f"scales_{first}", [P, count * P], U8)
+            quantize(codes[:], scales[:], joint_bf[:, block(first, count, P * PACK)])
+            for i in range(count):
+                operand[JOINT[JOINT.index(first) + i]] = (codes[:, i * P : (i + 1) * P], scales[:, i * P : (i + 1) * P])
 
+        round_w2(nc.scalar.copy, 0, slice(0, 4))
         for c in range(CHUNKS):
             round_hidden(c)
-        round_w2(0, slice(0, 4))
-        h0_codes = sbuf("h0_codes", [P, CHUNK], U32, tag="w2_raw0")
-        h0_scales = sbuf("h0_scales", [P, CHUNK], U8)
-        quantize(h0_codes[:], h0_scales[:], h0_bf[:])
-        round_w2(1, slice(0, 2))
-        round_w2(1, slice(2, 4))
-        quantize_joint("h1", 3)
+        round_w2(nc.vector.tensor_copy, 1, slice(0, 4))
+        quantize_hidden(0, 1, "w2_raw1")
+        round_w2(nc.vector.tensor_copy, 2, slice(0, 2))
+        round_w2(nc.vector.tensor_copy, 2, slice(2, 4))
+        quantize_joint("w0", 2)
+        quantize_hidden(1, 1, "w2_raw2")
         quantize_joint("w2", 2)
-        quantize_joint("h2", 2)
+        quantize_hidden(2, 2, "joint_bf")
 
         y = [sbuf(f"y{g}", [P, PACK, PAIR], F32) for g in range(2)]
         y_bf = sbuf("y_bf", [P, S, PACK], BF16)
@@ -143,12 +154,7 @@ def tile_picked_zgrn_relu_po_kernel(tc, x_words, x_scales, w1, w2, offs, out_0, 
         def gate_and_result(duo, c, bank):
             logits = psum.tile([P, 2, CHUNK], F32, name=f"logits{duo}{c}", tag=bank)
             for i in range(2):
-                w = block(f"w{2 * duo + i}")
-                if c == 0:
-                    product(logits[:, i, :], joint_codes[:, w], joint_scales[:, w], h0_codes[:], h0_scales[:])
-                else:
-                    a = block(f"h{c}")
-                    product(logits[:, i, :], joint_codes[:, w], joint_scales[:, w], joint_codes[:, a], joint_scales[:, a])
+                product(logits[:, i, :], *operand[f"w{2 * duo + i}"], *operand[f"h{c}"])
             gate = sbuf(f"gate{duo}{c}", [P, 2, CHUNK], F32)
             nc.scalar.activation(gate[:], logits[:], ACT.Sigmoid)
             ts = slice(2 * duo, 2 * duo + 2)

@@ -20,8 +20,8 @@ PACK = 4
 CHUNK = 128
 CHUNKS = S // CHUNK
 PAIR = 2 * CHUNK
-W2_ON_SCALAR = 32
-W2_EARLY = 88
+W2_ON_SCALAR = 16
+W2_EARLY = 64
 LAST_ON_SCALAR = 64
 
 JOINT = ["w0", "w1", "w2", "w3"]
@@ -55,7 +55,7 @@ def tile_picked_zgrn_relu_po_kernel(tc, x_words, x_scales, w1, w2, offs, out_0, 
             nc.sync.dma_start(out=scale_table[32 * q : 32 * q + 4, :].bitcast(I32), in_=x_scales[0, 4 * q : 4 * q + 4, :].bitcast(I32))
         nc.sync.dma_start(out=w1_raw[:, 2:4, :], in_=w1_rows[:, 2:4, :])
         nc.sync.dma_start(out=word_table[:].bitcast(I32), in_=x_words[0].rearrange("p n t -> p (n t)").bitcast(I32))
-        w2_parts = [(0, W2_ON_SCALAR), (W2_ON_SCALAR, W2_EARLY), (W2_EARLY, P)]
+        w2_parts = [(0, W2_EARLY), (W2_EARLY, P)]
         w2_raw = []
         for part, (lo, hi) in enumerate(w2_parts):
             w2_raw.append(sbuf(f"w2_raw{part}", [P, PACK, (hi - lo) * PACK], F32))
@@ -102,7 +102,7 @@ def tile_picked_zgrn_relu_po_kernel(tc, x_words, x_scales, w1, w2, offs, out_0, 
 
         joint_bf = sbuf("joint_bf", [P, len(JOINT) * P * PACK], BF16)
         operand = {}
-        h_bf = sbuf("h_bf", [P, S * PACK], BF16, tag="w2_raw0")
+        h_bf = sbuf("h_bf", [P, S * PACK], BF16, tag="warm_in")
 
         def block(name, count=1, width=P):
             at = JOINT.index(name)
@@ -119,11 +119,11 @@ def tile_picked_zgrn_relu_po_kernel(tc, x_words, x_scales, w1, w2, offs, out_0, 
             for i in range(count):
                 operand[f"h{first + i}"] = (codes[:, i * CHUNK : (i + 1) * CHUNK], scales[:, i * CHUNK : (i + 1) * CHUNK])
 
-        def round_w2(copy, part, tiles):
-            lo, hi = w2_parts[part]
-            dst = joint_bf[:, block("w0", PACK, P * PACK)].rearrange("p (t m j) -> p m j t", t=PACK, j=PACK)
+        def w2_views(part, lo, hi, tiles):
+            first = w2_parts[part][0]
+            dst = joint_bf[:].rearrange("p (t m j) -> p m j t", t=PACK, j=PACK)
             src = w2_raw[part][:].rearrange("p j (m t) -> p m j t", t=PACK)
-            copy(dst[:, lo:hi, :, tiles], src[:, :, :, tiles])
+            return dst[:, lo:hi, :, tiles], src[:, lo - first : hi - first, :, tiles]
 
         def quantize_joint(first, count):
             codes = sbuf(f"codes_{first}", [P, count * P], U32)
@@ -132,15 +132,15 @@ def tile_picked_zgrn_relu_po_kernel(tc, x_words, x_scales, w1, w2, offs, out_0, 
             for i in range(count):
                 operand[JOINT[JOINT.index(first) + i]] = (codes[:, i * P : (i + 1) * P], scales[:, i * P : (i + 1) * P])
 
-        round_w2(nc.scalar.copy, 0, slice(0, 4))
+        nc.scalar.activation(*w2_views(0, 0, W2_ON_SCALAR, slice(0, 4)), ACT.Identity, bias=warm_in[:])
         for c in range(CHUNKS):
             round_hidden(c)
-        round_w2(nc.vector.tensor_copy, 1, slice(0, 4))
-        quantize_hidden(0, 1, "w2_raw1")
-        round_w2(nc.vector.tensor_copy, 2, slice(0, 2))
-        round_w2(nc.vector.tensor_copy, 2, slice(2, 4))
+        nc.vector.tensor_copy(*w2_views(0, W2_ON_SCALAR, W2_EARLY, slice(0, 4)))
+        quantize_hidden(0, 1, "w2_raw0")
+        nc.vector.tensor_copy(*w2_views(1, W2_EARLY, P, slice(0, 2)))
+        nc.vector.tensor_copy(*w2_views(1, W2_EARLY, P, slice(2, 4)))
         quantize_joint("w0", 2)
-        quantize_hidden(1, 1, "w2_raw2")
+        quantize_hidden(1, 1, "w2_raw1")
         quantize_joint("w2", 2)
         quantize_hidden(2, 2, "joint_bf")
 

@@ -20,7 +20,7 @@ PACK = 4
 CHUNK = 128
 CHUNKS = S // CHUNK
 PAIR = 2 * CHUNK
-W2_ON_SCALAR = 16
+W2_ON_SCALAR = 24
 W2_EARLY = 64
 LAST_ON_SCALAR = 64
 
@@ -136,10 +136,10 @@ def tile_picked_zgrn_relu_po_kernel(tc, x_words, x_scales, w1, w2, offs, out_0, 
         for c in range(CHUNKS):
             round_hidden(c)
         nc.vector.tensor_copy(*w2_views(0, W2_ON_SCALAR, W2_EARLY, slice(0, 4)))
-        quantize_hidden(0, 1, "w2_raw0")
         nc.vector.tensor_copy(*w2_views(1, W2_EARLY, P, slice(0, 2)))
-        nc.vector.tensor_copy(*w2_views(1, W2_EARLY, P, slice(2, 4)))
+        quantize_hidden(0, 1, "w2_raw0")
         quantize_joint("w0", 2)
+        nc.vector.tensor_copy(*w2_views(1, W2_EARLY, P, slice(2, 4)))
         quantize_hidden(1, 1, "w2_raw1")
         quantize_joint("w2", 2)
         quantize_hidden(2, 2, "joint_bf")

@@ -90,8 +90,8 @@ def tile_picked_zgrn_relu_po_kernel(tc, x_words, x_scales, w1, w2, offs, out_0, 
         quantize_w1(0)
         gather_words(0, CHUNK)
         quantize_w1(1)
-        gather_words(CHUNK, PAIR)
-        gather_words(PAIR, S)
+        for c in range(1, CHUNKS):
+            gather_words(c * CHUNK, (c + 1) * CHUNK)
 
         pre = [psum.tile([P, PACK, CHUNK], F32, name=f"pre{c}") for c in range(CHUNKS)]
         for c in range(CHUNKS):
@@ -110,7 +110,7 @@ def tile_picked_zgrn_relu_po_kernel(tc, x_words, x_scales, w1, w2, offs, out_0, 
 
         def round_hidden(c):
             dst = h_bf[:, c * CHUNK * PACK : (c + 1) * CHUNK * PACK]
-            nc.scalar.activation(dst.rearrange("p (n t) -> p n t", t=PACK), pre[c][:].rearrange("p t n -> p n t"), ACT.Relu)
+            nc.scalar.activation(dst.rearrange("p (g i t) -> p g t i", i=2, t=PACK), pre[c][:].rearrange("p t (g i) -> p g t i", i=2), ACT.Relu)
 
         def quantize_hidden(first, count, slot):
             codes = sbuf(f"h_codes{first}", [P, count * CHUNK], U32, tag=slot)

@@ -49,11 +49,11 @@ def tile_picked_zgrn_relu_po_kernel(tc, x_words, x_scales, w1, w2, offs, out_0, 
         w1_rows = w1.rearrange("(p j) c -> p j c", j=PACK)
         w2_rows = w2.rearrange("(p j) c -> p j c", j=PACK)
         nc.vector.memset(scale_table[:].bitcast(I32), 0)
-        nc.sync.dma_start(out=w1_raw[:, 0:2, :], in_=w1_rows[:, 0:2, :])
+        nc.sync.dma_start(out=w1_raw[:, :, : H // 2], in_=w1_rows[:, :, : H // 2])
         nc.sync.dma_start(offsets[:], offs)
         for q in range(4):
             nc.sync.dma_start(out=scale_table[32 * q : 32 * q + 4, :].bitcast(I32), in_=x_scales[0, 4 * q : 4 * q + 4, :].bitcast(I32))
-        nc.sync.dma_start(out=w1_raw[:, 2:4, :], in_=w1_rows[:, 2:4, :])
+        nc.sync.dma_start(out=w1_raw[:, :, H // 2 :], in_=w1_rows[:, :, H // 2 :])
         nc.sync.dma_start(out=word_table[:].bitcast(I32), in_=x_words[0].rearrange("p n t -> p (n t)").bitcast(I32))
         w2_parts = [(0, W2_EARLY), (W2_EARLY, P)]
         w2_raw = []
@@ -74,9 +74,9 @@ def tile_picked_zgrn_relu_po_kernel(tc, x_words, x_scales, w1, w2, offs, out_0, 
         w1_codes = [sbuf(f"w1_codes{duo}", [P, 2 * P], U32) for duo in range(2)]
         w1_scales = [sbuf(f"w1_scales{duo}", [P, 2 * P], U8) for duo in range(2)]
 
-        def w1_views(duo, rows):
-            src = w1_raw[:].rearrange("p j (m t) -> p m j t", t=PACK)[:, :, rows, 2 * duo : 2 * duo + 2]
-            return w1_dealt[duo][:].rearrange("p t m j -> p m j t")[:, :, rows], src
+        def w1_views(duo, lo, hi):
+            src = w1_raw[:].rearrange("p j (m t) -> p m j t", t=PACK)[:, lo:hi, :, 2 * duo : 2 * duo + 2]
+            return w1_dealt[duo][:].rearrange("p t m j -> p m j t")[:, lo:hi], src
 
         def quantize_w1(duo):
             quantize(w1_codes[duo][:], w1_scales[duo][:], w1_dealt[duo][:].rearrange("p t m j -> p (t m j)"))
@@ -84,9 +84,9 @@ def tile_picked_zgrn_relu_po_kernel(tc, x_words, x_scales, w1, w2, offs, out_0, 
         def gather_words(lo, hi):
             nc.vector.tensor_copy(x_codes[:, lo:hi], word_table[:].indirect(offsets[:, lo // 16 : hi // 16]))
 
-        nc.scalar.copy(*w1_views(0, slice(0, 2)))
-        nc.vector.tensor_copy(*w1_views(0, slice(2, 4)))
-        nc.scalar.copy(*w1_views(1, slice(0, 4)))
+        nc.scalar.copy(*w1_views(0, 0, P // 2))
+        nc.vector.tensor_copy(*w1_views(0, P // 2, P))
+        nc.scalar.copy(*w1_views(1, 0, P))
         quantize_w1(0)
         gather_words(0, CHUNK)
         quantize_w1(1)

from contextlib import ExitStack

import concourse.mybir as mybir

K, T, S, H = 512, 1024, 512, 512
FLOPS = 2 * 2 * K * H * S

F32 = mybir.dt.float32
BF16 = mybir.dt.bfloat16
I32 = mybir.dt.int32
U32 = mybir.dt.uint32
U16 = mybir.dt.uint16
U8 = mybir.dt.uint8
FP8X4 = mybir.dt.float8_e4m3fn_x4
ACT = mybir.ActivationFunctionType
ALU = mybir.AluOpType

P = 128
PACK = 4
CHUNK = 128
CHUNKS = S // CHUNK
PAIR = 2 * CHUNK
W2_ON_SCALAR = 24
W2_EARLY = 64
LAST_ON_SCALAR = 64

JOINT = ["w0", "w1", "w2", "w3"]


def tile_picked_zgrn_relu_po_kernel(tc, x_words, x_scales, w1, w2, offs, out_0, out_1, out_2):
    nc = tc.nc
    with ExitStack() as ctx:
        keep = ctx.enter_context(tc.tile_pool(name="keep", bufs=1))
        psum = ctx.enter_context(tc.psum_pool(name="psum", bufs=1))

        def sbuf(name, shape, dtype, tag=None):
            return keep.tile(shape, dtype, name=name, tag=tag or name, align_bytes=64)

        def quantize(codes, scales, values):
            nc.vector.quantize_mx(out=codes.bitcast(FP8X4), scales=scales, in_=values)

        def product(out, w_codes, w_scales, a_codes, a_scales):
            nc.tensor.matmul_mx(out=out, lhsT=w_codes.bitcast(FP8X4), lhsT_scale=w_scales, rhs=a_codes.bitcast(FP8X4), rhs_scale=a_scales, start=True, stop=True)

        offsets = keep.tile([P, S // 16], U16, name="offsets")
        word_table = sbuf("word_table", [P, T], U32)
        scale_table = sbuf("scale_table", [P, T], U8)
        w1_raw = sbuf("w1_raw", [P, PACK, H], F32)
        w1_rows = w1.rearrange("(p j) c -> p j c", j=PACK)
        w2_rows = w2.rearrange("(p j) c -> p j c", j=PACK)
        nc.vector.memset(scale_table[:].bitcast(I32), 0)
        nc.sync.dma_start(out=w1_raw[:, :, : H // 2], in_=w1_rows[:, :, : H // 2])
        nc.sync.dma_start(offsets[:], offs)
        for q in range(4):
            nc.sync.dma_start(out=scale_table[32 * q : 32 * q + 4, :].bitcast(I32), in_=x_scales[0, 4 * q : 4 * q + 4, :].bitcast(I32))
        nc.sync.dma_start(out=w1_raw[:, :, H // 2 :], in_=w1_rows[:, :, H // 2 :])
        nc.sync.dma_start(out=word_table[:].bitcast(I32), in_=x_words[0].rearrange("p n t -> p (n t)").bitcast(I32))
        w2_parts = [(0, W2_EARLY), (W2_EARLY, P)]
        w2_raw = []
        for part, (lo, hi) in enumerate(w2_parts):
            w2_raw.append(sbuf(f"w2_raw{part}", [P, PACK, (hi - lo) * PACK], F32))
            nc.sync.dma_start(out=w2_raw[part][:], in_=w2_rows[:, :, lo * PACK : hi * PACK])

        warm_in = sbuf("warm_in", [P, 1], F32)
        warm_out = sbuf("warm_out", [P, 1], F32)
        nc.vector.memset(warm_in[:], 0.0)
        nc.scalar.activation(warm_out[:], warm_in[:], ACT.Sigmoid)

        x_bytes = sbuf("x_bytes", [P, S], U8)
        x_codes = sbuf("x_codes", [P, S], U32)
        nc.vector.tensor_copy(x_bytes[:], scale_table[:].indirect(offsets[:]))

        w1_dealt = [sbuf(f"w1_dealt{duo}", [P, 2, P, PACK], BF16) for duo in range(2)]
        w1_codes = [sbuf(f"w1_codes{duo}", [P, 2 * P], U32) for duo in range(2)]
        w1_scales = [sbuf(f"w1_scales{duo}", [P, 2 * P], U8) for duo in range(2)]

        def w1_views(duo, lo, hi):
            src = w1_raw[:].rearrange("p j (m t) -> p m j t", t=PACK)[:, lo:hi, :, 2 * duo : 2 * duo + 2]
            return w1_dealt[duo][:].rearrange("p t m j -> p m j t")[:, lo:hi], src

        def quantize_w1(duo):
            quantize(w1_codes[duo][:], w1_scales[duo][:], w1_dealt[duo][:].rearrange("p t m j -> p (t m j)"))

        def gather_words(lo, hi):
            nc.vector.tensor_copy(x_codes[:, lo:hi], word_table[:].indirect(offsets[:, lo // 16 : hi // 16]))

        nc.scalar.copy(*w1_views(0, 0, P // 2))
        nc.vector.tensor_copy(*w1_views(0, P // 2, P))
        nc.scalar.copy(*w1_views(1, 0, P))
        quantize_w1(0)
        gather_words(0, CHUNK)
        quantize_w1(1)
        for c in range(1, CHUNKS):
            gather_words(c * CHUNK, (c + 1) * CHUNK)

        pre = [psum.tile([P, PACK, CHUNK], F32, name=f"pre{c}") for c in range(CHUNKS)]
        for c in range(CHUNKS):
            cols = slice(c * CHUNK, (c + 1) * CHUNK)
            for t in range(PACK):
                wcols = slice((t % 2) * P, (t % 2 + 1) * P)
                product(pre[c][:, t, :], w1_codes[t // 2][:, wcols], w1_scales[t // 2][:, wcols], x_codes[:, cols], x_bytes[:, cols])

        joint_bf = sbuf("joint_bf", [P, len(JOINT) * P * PACK], BF16)
        operand = {}
        h_bf = sbuf("h_bf", [P, S * PACK], BF16, tag="warm_in")

        def block(name, count=1, width=P):
            at = JOINT.index(name)
            return slice(at * width, (at + count) * width)

        def round_hidden(c):
            dst = h_bf[:, c * CHUNK * PACK : (c + 1) * CHUNK * PACK]
            nc.scalar.activation(dst.rearrange("p (g i t) -> p g t i", i=2, t=PACK), pre[c][:].rearrange("p t (g i) -> p g t i", i=2), ACT.Relu)

        def quantize_hidden(first, count, slot):
            codes = sbuf(f"h_codes{first}", [P, count * CHUNK], U32, tag=slot)
            scales = sbuf(f"h_scales{first}", [P, count * CHUNK], U8)
            quantize(codes[:], scales[:], h_bf[:, first * CHUNK * PACK : (first + count) * CHUNK * PACK])
            for i in range(count):
                operand[f"h{first + i}"] = (codes[:, i * CHUNK : (i + 1) * CHUNK], scales[:, i * CHUNK : (i + 1) * CHUNK])

        def w2_views(part, lo, hi, tiles):
            first = w2_parts[part][0]
            dst = joint_bf[:].rearrange("p (t m j) -> p m j t", t=PACK, j=PACK)
            src = w2_raw[part][:].rearrange("p j (m t) -> p m j t", t=PACK)
            return dst[:, lo:hi, :, tiles], src[:, lo - first : hi - first, :, tiles]

        def quantize_joint(first, count):
            codes = sbuf(f"codes_{first}", [P, count * P], U32)
            scales = sbuf(f"scales_{first}", [P, count * P], U8)
            quantize(codes[:], scales[:], joint_bf[:, block(first, count, P * PACK)])
            for i in range(count):
                operand[JOINT[JOINT.index(first) + i]] = (codes[:, i * P : (i + 1) * P], scales[:, i * P : (i + 1) * P])

        nc.scalar.activation(*w2_views(0, 0, W2_ON_SCALAR, slice(0, 4)), ACT.Identity, bias=warm_in[:])
        for c in range(CHUNKS):
            round_hidden(c)
        nc.vector.tensor_copy(*w2_views(0, W2_ON_SCALAR, W2_EARLY, slice(0, 4)))
        nc.vector.tensor_copy(*w2_views(1, W2_EARLY, P, slice(0, 2)))
        quantize_hidden(0, 1, "w2_raw0")
        quantize_joint("w0", 2)
        nc.vector.tensor_copy(*w2_views(1, W2_EARLY, P, slice(2, 4)))
        quantize_hidden(1, 1, "w2_raw1")
        quantize_joint("w2", 2)
        quantize_hidden(2, 2, "joint_bf")

        y = [sbuf(f"y{g}", [P, PACK, PAIR], F32) for g in range(2)]
        y_bf = sbuf("y_bf", [P, S, PACK], BF16)
        y_codes = sbuf("y_codes", [P, S], U32)
        y_scales = sbuf("y_scales", [P, S], U8)
        y_rows = out_0.rearrange("(p t) n -> p t n", t=PACK)
        word_rows = out_1[0].rearrange("p n t -> p (n t)").bitcast(I32)

        def gate_and_result(duo, c, bank):
            logits = psum.tile([P, 2, CHUNK], F32, name=f"logits{duo}{c}", tag=bank)
            for i in range(2):
                product(logits[:, i, :], *operand[f"w{2 * duo + i}"], *operand[f"h{c}"])
            gate = sbuf(f"gate{duo}{c}", [P, 2, CHUNK], F32)
            nc.scalar.activation(gate[:], logits[:], ACT.Sigmoid)
            ts = slice(2 * duo, 2 * duo + 2)
            nc.vector.scalar_tensor_tensor(y[c // 2][:, ts, (c % 2) * CHUNK : (c % 2 + 1) * CHUNK], pre[c][:, ts, :], 0.0, gate[:], ALU.max, ALU.mult)

        banks = ["logits_a", "logits_b", "logits_c", "logits_d"]
        for g in range(2):
            for duo in range(2):
                for i in range(2):
                    gate_and_result(duo, 2 * g + i, banks[2 * duo + i])
                ts = slice(2 * duo, 2 * duo + 2)
                nc.sync.dma_start(out=y_rows[:, ts, g * PAIR : (g + 1) * PAIR], in_=y[g][:, ts, :])

        def result_views(lo, hi):
            g = lo // PAIR
            return y_bf[:, lo:hi, :], y[g][:, :, lo - g * PAIR : hi - g * PAIR]

        def by_fours(lo, hi):
            dst, src = result_views(lo, hi)
            return dst.rearrange("p (g i) t -> p g t i", i=4), src.rearrange("p t (g i) -> p g t i", i=4)

        dst, src = result_views(0, CHUNK)
        nc.gpsimd.tensor_scalar(dst, src.rearrange("p t n -> p n t"), 1.0, 0.0, ALU.mult, ALU.add)
        nc.scalar.copy(*by_fours(CHUNK, PAIR))
        nc.vector.tensor_copy(*by_fours(PAIR, PAIR + CHUNK))
        nc.vector.tensor_copy(*by_fours(PAIR + CHUNK, S - LAST_ON_SCALAR))
        nc.scalar.copy(*by_fours(S - LAST_ON_SCALAR, S))
        for g in range(2):
            cols = slice(g * PAIR, (g + 1) * PAIR)
            quantize(y_codes[:, cols], y_scales[:, cols], y_bf[:, cols, :].rearrange("p n t -> p (n t)"))
            nc.sync.dma_start(out=word_rows[:, cols], in_=y_codes[:, cols].bitcast(I32))
        for q in range(4):
            queue = nc.scalar if q % 2 == 0 else nc.sync
            queue.dma_start(out=out_2[0, 4 * q : 4 * q + 4, :].bitcast(I32), in_=y_scales[32 * q : 32 * q + 4, :].bitcast(I32))
